import numpy as np
import ml_dtypes


def mxq(x, axis, fmt="e4m3"):
    dtype, down = {"e4m3": (ml_dtypes.float8_e4m3fn, 7), "e5m2": (ml_dtypes.float8_e5m2, 14)}[fmt]
    v = np.moveaxis(np.asarray(x, np.float32).astype(ml_dtypes.bfloat16).astype(np.float64), axis, -1)
    blocks = v.reshape(v.shape[:-1] + (-1, 32))
    amax = np.abs(blocks).max(-1, keepdims=True)
    byte = np.maximum(np.where(amax > 0, np.frexp(amax)[1] - 1 + 127, 0) - down, 1)
    scale = np.exp2(byte - 127.0)
    codes = (blocks / scale).astype(np.float32).astype(dtype).astype(np.float64)
    return np.moveaxis((codes * scale).reshape(v.shape), -1, axis)


WIDE = False


def mx_kscale(k):
    if not WIDE:
        return np.ones(k)
    levels = np.array([10, -10, 5, -5, 0])
    if k % 512:
        return np.exp2(np.random.permutation(np.resize(levels, k // 32))).repeat(32)
    a = np.empty((k // 512, 16))
    for p in range(k // 512):
        a[p, :8] = np.random.permutation(np.resize(levels, 8))
        for g in range(8):
            far = levels[np.abs(levels - a[p, g]) >= 10]
            a[p, g + 8] = far[np.random.randint(len(far))]
    return np.exp2(a.ravel()).repeat(32)


BF16 = ml_dtypes.bfloat16


def bf(x):
    return np.asarray(x, np.float32).astype(BF16)


def f64(x):
    return np.asarray(x).astype(np.float64)


T, K, D, P, R = 1024, 1024, 1024, 1024, 128


def draw0():
    s = mx_kscale(K)
    u = mx_kscale(T)
    v = mx_kscale(T)
    return {"x": bf(np.random.standard_normal((T, K)) * s),
            "w_head": bf(np.random.standard_normal((K, D)) / np.sqrt(K) / s[:, None]),
            "b_head": bf(0.3 * np.random.standard_normal(D)),
            "g_head": bf(np.random.uniform(0.5, 1.5, T) * u),
            "a_head": bf(np.random.standard_normal((P, T)) / np.sqrt(T) / u),
            "w_tail": bf(np.random.standard_normal((K, D)) / np.sqrt(K) / s[:, None]),
            "b_tail": bf(0.3 * np.random.standard_normal(D)),
            "g_tail": bf(np.random.uniform(0.5, 1.5, T) * v),
            "a_tail": bf(np.random.standard_normal((P, T)) / np.sqrt(T) / v),
            "rel": bf(np.random.standard_normal((R, D // R)) / np.sqrt(D // R)),
            "beta": bf(0.2 * np.random.standard_normal(R))}


def core(x, w_head, b_head, g_head, a_head, w_tail, b_tail, g_tail, a_tail, rel, beta):
    xq = mxq(f64(x), 1, "e4m3")
    h = np.tanh((xq @ mxq(f64(w_head), 0, "e4m3")) + f64(b_head)) * f64(g_head)[:, None]
    t = np.tanh((xq @ mxq(f64(w_tail), 0, "e4m3")) + f64(b_tail)) * f64(g_tail)[:, None]
    eh = mxq(f64(a_head), 1, "e4m3") @ mxq(h, 0, "e4m3")
    et = mxq(f64(a_tail), 1, "e4m3") @ mxq(t, 0, "e4m3")
    return ((eh * et).reshape(P, R, D // R) * f64(rel)).sum(axis=2) + f64(beta)


def e4m3fn_bytes(y):
    return np.clip(np.asarray(y, np.float64), -448.0, 448.0).astype(np.float32).astype(ml_dtypes.float8_e4m3fn).view(np.uint8)


def e4m3fn_values(b):
    return np.asarray(b, np.uint8).view(ml_dtypes.float8_e4m3fn).astype(np.float64)


def setup_inputs():
    d = draw0()
    x0 = np.asarray(d['x']).astype(np.float64)
    s = (np.max(np.abs(x0), axis=(0,), keepdims=True) / 448.0).astype(np.float32)
    out = {}
    for k, v in d.items():
        if k == 'x':
            out['x_bytes'] = e4m3fn_bytes(x0 / s.astype(np.float64))
            out['x_scale'] = s
        else:
            out[k] = v
    return out


def reference(x_bytes, x_scale, w_head, b_head, g_head, a_head, w_tail, b_tail, g_tail, a_tail, rel, beta):
    return core(e4m3fn_values(x_bytes) * x_scale.astype(np.float64), w_head, b_head, g_head, a_head, w_tail, b_tail, g_tail, a_tail, rel, beta)

@@ -1,0 +1,321 @@
+from contextlib import ExitStack
+
+import concourse.mybir as mybir
+from concourse.masks import make_identity
+
+T, K, D, P, R = 1024, 1024, 1024, 1024, 128
+C = D // R
+FLOPS = 4 * 2 * 1024 * 1024 * 1024
+
+F32 = mybir.dt.float32
+BF16 = mybir.dt.bfloat16
+U32 = mybir.dt.uint32
+U8 = mybir.dt.uint8
+FP8 = mybir.dt.float8_e4m3fn
+FP8X4 = mybir.dt.float8_e4m3fn_x4
+ACT = mybir.ActivationFunctionType
+ALU = mybir.AluOpType
+
+
+def tile_relation_trilinear_score_f4_kernel(
+    tc, x_bytes, x_scale, w_head, b_head, g_head, a_head, w_tail, b_tail, g_tail, a_tail, rel, beta, out
+):
+    nc = tc.nc
+    w_in = (w_head, w_tail)
+    a_in = (a_head, a_tail)
+    g_in = (g_head, g_tail)
+
+    with ExitStack() as ctx:
+        keep = ctx.enter_context(tc.tile_pool(name="keep", bufs=1))
+        work = ctx.enter_context(tc.tile_pool(name="work", bufs=2))
+        psum = ctx.enter_context(tc.psum_pool(name="psum", bufs=4))
+
+        scale_bc = keep.tile([128, K], F32, name="scale_bc")
+        nc.scalar.dma_start(out=scale_bc[:], in_=x_scale.rearrange("o k -> (o k)").partition_broadcast(128))
+
+        warm = keep.tile([128, 1], F32, name="warm")
+        nc.vector.memset(warm[:], 0.0)
+        nc.scalar.activation(out=warm[:], in_=warm[:], func=ACT.Tanh)
+
+        vecs = keep.tile([128, 128], BF16, name="vecs")
+        nc.vector.memset(vecs[:], 0.0)
+        nc.scalar.dma_start(out=vecs[0:8, :], in_=b_head.rearrange("(t q) -> t q", q=128))
+        nc.scalar.dma_start(out=vecs[8:16, :], in_=b_tail.rearrange("(t q) -> t q", q=128))
+
+        x_raw = []
+        x_view = x_bytes.rearrange("(g p j) k -> g p j k", p=128, j=4)
+        for g in range(2):
+            xb = keep.tile([128, 4, K], U8, name="x_raw%d" % g)
+            x_raw.append(xb)
+
+        w_raw = {}
+        a_raw = {}
+
+        def load_x(g, j0, j1):
+            nc.sync.dma_start(out=x_raw[g][:, j0:j1, :], in_=x_view[g, :, j0:j1, :])
+
+        def load_w(role, kk, dh):
+            t = work.tile([128, 4, 512], BF16, name="raw", tag="raw", bufs=9, align_bytes=64)
+            view = w_in[role][kk * 512:(kk + 1) * 512, dh * 512:(dh + 1) * 512]
+            nc.sync.dma_start(out=t[:], in_=view.rearrange("(p j) d -> p j d", j=4))
+            w_raw[role, kk, dh] = t
+
+        def load_a(role, pp):
+            t = work.tile([128, 2, T], BF16, name="raw", tag="raw", bufs=9, align_bytes=64)
+            view = a_in[role][pp * 256:(pp + 1) * 256, :]
+            nc.sync.dma_start(out=t[:], in_=view.rearrange("(s p) t -> p s t", p=128))
+            a_raw[role, pp] = t
+
+        load_x(0, 0, 2)
+        load_x(0, 2, 4)
+        load_w(0, 0, 0)
+        load_w(0, 1, 0)
+        load_x(1, 0, 4)
+        load_w(0, 0, 1)
+        load_w(0, 1, 1)
+
+        ident = keep.tile([128, 128], F32, name="ident")
+        make_identity(nc, ident[:])
+        ident_bf = keep.tile([128, 128], BF16, name="ident_bf")
+        make_identity(nc, ident_bf[:])
+
+        g_sb = []
+        for role in range(2):
+            gain_sb = keep.tile([128, 2, 4], BF16, name="gain_sb%d" % role)
+            nc.scalar.dma_start(out=gain_sb[:], in_=g_in[role].rearrange("(g p j) -> p g j", p=128, j=4))
+            g_sb.append(gain_sb)
+        rel_bf = keep.tile([128, C], BF16, name="rel_bf")
+        nc.scalar.dma_start(out=rel_bf[:], in_=rel)
+        beta_bc = keep.tile([128, R], BF16, name="beta_bc")
+        nc.scalar.dma_start(out=beta_bc[:], in_=beta.partition_broadcast(128))
+
+        xq = {}
+        wq = {}
+        aq = {}
+        hq = {}
+        hg = {}
+        xg = {}
+        ag = {}
+        wg = {}
+        th = {}
+        ehs = {}
+        prod = {}
+
+        def new_codes(pool, nm):
+            codes = pool.tile([128, 512], U32, name=nm + "_codes", align_bytes=64)
+            scales = pool.tile([128, 512], U8, name=nm + "_scales", align_bytes=64)
+            return codes, scales
+
+        def quantize(dst, src):
+            nc.vector.quantize_mx(out=dst[0][:].bitcast(FP8X4), scales=dst[1][:], in_=src)
+
+        def mx(acc, lhs, lcols, rhs, start, stop):
+            nc.tensor.matmul_mx(
+                out=acc,
+                lhsT=lhs[0][:, lcols].bitcast(FP8X4),
+                lhsT_scale=lhs[1][:, lcols],
+                rhs=rhs[0][:].bitcast(FP8X4),
+                rhs_scale=rhs[1][:],
+                start=start,
+                stop=stop,
+            )
+
+        def copy(eng, out_ap, in_ap):
+            if eng == "s":
+                nc.scalar.copy(out=out_ap, in_=in_ap)
+            else:
+                nc.vector.tensor_copy(out=out_ap, in_=in_ap)
+
+        def x_tile(g, j, eng="s"):
+            xs = work.tile([128, K], BF16, name="xs", tag="xs", bufs=2, align_bytes=64)
+            nc.vector.tensor_tensor(out=xs[:], in0=x_raw[g][:, j, :].bitcast(FP8), in1=scale_bc[:], op=ALU.mult)
+            words = xs[:].bitcast(F32)
+            bank = psum.tile([128, 2, 2, 128], F32, name="tr", tag="tr", bufs=4)
+            for kk in range(2):
+                for u in range(2):
+                    nc.tensor.transpose(bank[:, kk, u, :], words[:, 256 * kk + u:256 * (kk + 1):2], ident[:])
+            if j == 0:
+                xg[g] = work.tile([128, 2, 512, 4], BF16, name="xg", tag="xg", bufs=1, align_bytes=64)
+            dst = xg[g][:].rearrange("p k n t -> p (k n t)").bitcast(F32)
+            dst = dst.rearrange("p (k n u) -> p k n u", k=2, u=2)[:, :, 128 * j:128 * (j + 1), :]
+            copy(eng, dst, bank[:].rearrange("p k u r -> p k r u"))
+
+        def x_quant(g, kk):
+            xq[g, kk] = new_codes(keep, "xq%d%d" % (g, kk))
+            quantize(xq[g, kk], xg[g][:, kk].rearrange("p n t -> p (n t)"))
+
+        def w_il(role, kk, dh, eng):
+            t = work.tile([128, 512, 4], BF16, name="grp", tag="grp", bufs=5, align_bytes=64)
+            copy(eng, t[:], w_raw[role, kk, dh][:].rearrange("p j d -> p d j"))
+            wg[role, kk, dh] = t
+
+        def w_quant(role, kk, dh):
+            wq[role, kk, dh] = new_codes(keep, "wq%d%d%d" % (role, kk, dh))
+            quantize(wq[role, kk, dh], wg[role, kk, dh][:].rearrange("p d j -> p (d j)"))
+
+        def a_bank(role, g, pp, eng):
+            words = a_raw[role, pp][:].rearrange("p s t -> p (s t)").bitcast(F32)
+            bank = psum.tile([128, 2, 2, 128], F32, name="tr", tag="tr", bufs=4)
+            for s in range(2):
+                for u in range(2):
+                    w0 = 512 * s + 256 * g
+                    nc.tensor.transpose(bank[:, s, u, :], words[:, w0 + u:w0 + 256:2], ident[:])
+            ph = pp // 2
+            if (role, g, ph) not in ag:
+                ag[role, g, ph] = work.tile([128, 512, 4], BF16, name="grp", tag="grp", bufs=5, align_bytes=64)
+            dst = ag[role, g, ph][:].rearrange("p n t -> p (n t)").bitcast(F32)
+            dst = dst.rearrange("p (s r u) -> p s r u", s=4, u=2)[:, 2 * (pp % 2):2 * (pp % 2) + 2]
+            copy(eng, dst, bank[:].rearrange("p s u r -> p s r u"))
+
+        def a_quant(role, g, ph):
+            aq[role, g, ph] = new_codes(keep, "aq%d%d%d" % (role, g, ph))
+            quantize(aq[role, g, ph], ag[role, g, ph][:].rearrange("p n t -> p (n t)"))
+
+        def unit_mm(role, g, dt):
+            acc = psum.tile([128, 512], F32, name="mm", tag="mm", bufs=4)
+            cols = slice(128 * (dt % 4), 128 * (dt % 4 + 1))
+            for kk in range(2):
+                mx(acc[:], wq[role, kk, dt // 4], cols, xq[g, kk], kk == 0, kk == 1)
+            t = work.tile([128, 512], F32, name="th", tag="th", bufs=4)
+            nc.scalar.activation(out=t[:], in_=acc[:], func=ACT.Tanh, bias=b_t[:, 8 * role + dt:8 * role + dt + 1])
+            th[role, g, dt] = t
+
+        def unit_tr(role, g, dt):
+            t = th[role, g, dt]
+            bank = psum.tile([128, 4, 128], F32, name="tr", tag="tr", bufs=4)
+            for j in range(4):
+                nc.tensor.transpose(bank[:, j, :], t[:, 128 * j:128 * (j + 1)], ident[:])
+            if dt == 0:
+                hg[role, g] = work.tile([128, C, 128, 4], BF16, name="hg", tag="hg", bufs=2, align_bytes=64)
+            gain = g_sb[role][:, g, :].unsqueeze(1).unsqueeze(1).to_broadcast([128, C, 16, 4])
+            nc.vector.tensor_tensor(
+                out=hg[role, g][:, :, 16 * dt:16 * (dt + 1), :],
+                in0=bank[:].rearrange("p j (r c) -> p c r j", c=C),
+                in1=gain,
+                op=ALU.mult,
+            )
+
+        def h_quant(role, g, ch):
+            hq[role, g, ch] = new_codes(keep, "hq%d%d%d" % (role, g, ch))
+            quantize(hq[role, g, ch], hg[role, g][:, 4 * ch:4 * ch + 4].rearrange("p c r t -> p (c r t)"))
+
+        def pooled(role, c, ph):
+            acc = psum.tile([128, 512], F32, name="mm", tag="mm", bufs=4)
+            cols = slice(128 * (c % 4), 128 * (c % 4 + 1))
+            for g in range(2):
+                mx(acc[:], hq[role, g, c // 4], cols, aq[role, g, ph], g == 0, g == 1)
+            return acc
+
+        def eh(c, ph):
+            acc = pooled(0, c, ph)
+            t = work.tile([128, 512], F32, name="ehs", tag="ehs", bufs=16)
+            nc.scalar.activation(out=t[:], in_=acc[:], func=ACT.Copy, scale=rel_f[:, c:c + 1])
+            ehs[c, ph] = t
+
+        def et(c, ph):
+            acc = pooled(1, c, ph)
+            t = work.tile([128, 512], F32, name="prod", tag="prod", bufs=5)
+            nc.vector.tensor_tensor(out=t[:], in0=acc[:], in1=ehs[c, ph][:], op=ALU.mult)
+            prod[c, ph] = t
+
+        score = {}
+
+        def sum_tr(c, ph):
+            for m in range(4):
+                if c == 0:
+                    score[ph, m] = psum.tile([128, 128], F32, name="tr", tag="tr", bufs=4)
+                nc.tensor.matmul(
+                    score[ph, m][:],
+                    lhsT=prod[c, ph][:, 128 * m:128 * (m + 1)],
+                    rhs=ident[:],
+                    is_transpose=True,
+                    start=(c == 0),
+                    stop=(c == C - 1),
+                )
+
+        def finish(ph):
+            o = work.tile([128, 4, R], F32, name="o", tag="o", bufs=2)
+            for m in range(4):
+                nc.vector.tensor_tensor(out=o[:, m, :], in0=score[ph, m][:], in1=beta_bc[:], op=ALU.add)
+            nc.sync.dma_start(out=out[512 * ph:512 * (ph + 1), :].rearrange("(m p) r -> p m r", p=128), in_=o[:])
+
+        rel_f = keep.tile([128, C], F32, name="rel_f")
+        nc.vector.tensor_copy(out=rel_f[:], in_=rel_bf[:])
+        b_ps = psum.tile([128, 128], BF16, name="tr", tag="tr", bufs=4)
+        nc.tensor.transpose(b_ps[:], vecs[:], ident_bf[:])
+        b_t = keep.tile([128, 16], BF16, name="b_t")
+        nc.vector.tensor_copy(out=b_t[:], in_=b_ps[:, 0:16])
+
+        for j in range(4):
+            x_tile(0, j)
+        w_il(0, 0, 0, "s")
+        w_il(0, 1, 0, "v")
+        x_quant(0, 0)
+        x_quant(0, 1)
+        w_quant(0, 0, 0)
+        w_quant(0, 1, 0)
+
+        for pp in range(4):
+            load_a(0, pp)
+        for dh in range(2):
+            for kk in range(2):
+                load_w(1, kk, dh)
+        for pp in range(4):
+            load_a(1, pp)
+
+        groups = [(role, g, dt) for role in range(2) for g in range(2) for dt in range(0, 8, 2)]
+        for i in range(len(groups) + 1):
+            if i < len(groups):
+                role, g, dt = groups[i]
+                unit_mm(role, g, dt)
+                unit_mm(role, g, dt + 1)
+            if i > 0:
+                role, g, dt = groups[i - 1]
+                unit_tr(role, g, dt)
+                unit_tr(role, g, dt + 1)
+                if dt == 6:
+                    h_quant(role, g, 0)
+                    h_quant(role, g, 1)
+            if i == 0:
+                x_tile(1, 0)
+                x_tile(1, 1)
+                w_il(0, 0, 1, "s")
+                w_il(0, 1, 1, "s")
+            if i == 1:
+                w_quant(0, 0, 1)
+                w_quant(0, 1, 1)
+                x_tile(1, 2)
+                x_tile(1, 3)
+            if i == 2:
+                x_quant(1, 0)
+                x_quant(1, 1)
+            if 4 <= i < 8:
+                pp = i - 4
+                a_bank(0, 0, pp, "s")
+                a_bank(0, 1, pp, "s")
+                if pp % 2 == 1:
+                    a_quant(0, 0, pp // 2)
+                    a_quant(0, 1, pp // 2)
+            if 4 <= i < 8:
+                kk, dh = i % 2, (i - 4) // 2
+                w_il(1, kk, dh, "v" if kk else "s")
+                w_quant(1, kk, dh)
+            if 8 <= i < 16:
+                pp, g = (i - 8) // 2, i % 2
+                a_bank(1, g, pp, "v")
+                if pp % 2 == 1:
+                    a_quant(1, g, pp // 2)
+            if 10 <= i:
+                first = 2 * (i - 10)
+                for n in range(first, first + (2 if i < 16 else 4)):
+                    eh(n % 8, n // 8)
+
+        pairs = [(ph, c) for ph in range(2) for c in range(C)]
+        for n in range(len(pairs) + 2):
+            if n < len(pairs):
+                et(pairs[n][1], pairs[n][0])
+            if n >= 2:
+                ph, c = pairs[n - 2]
+                sum_tr(c, ph)
+                if c == C - 1:
+                    finish(ph)

@@ -16,6 +16,17 @@ FP8X4 = mybir.dt.float8_e4m3fn_x4
 ACT = mybir.ActivationFunctionType
 ALU = mybir.AluOpType
 
+X_PRE = 2
+X1_SLOT = 0
+EH_SLOT = (11, 11, 11, 11, 11, 12, 13, 14, 14, 14, 15, 15, 15, 17, 17, 17)
+TT_ENG = "SSSVSSSSSVVVSSSSSV"
+AT_SLOT = (0, 1, 1, 3, 5, 8, 9, 10, 3, 5, 5, 7, 7, 10, 14, 15)
+AC_ENG = "VSSVSSVVVSSVSVSS"
+W_SLOT = ((None, None, 0, 0), (3, 5, 7, 8))
+W_ENG = ("SV", "VS")
+AQ_LAG = 2
+SUM_RUNS = (4, 4, 4, 4)
+
 
 def tile_relation_trilinear_score_f4_kernel(
     tc, x_bytes, x_scale, w_head, b_head, g_head, a_head, w_tail, b_tail, g_tail, a_tail, rel, beta, out
@@ -24,6 +35,7 @@ def tile_relation_trilinear_score_f4_kernel(
     w_in = (w_head, w_tail)
     a_in = (a_head, a_tail)
     g_in = (g_head, g_tail)
+    b_in = (b_head, b_tail)
 
     with ExitStack() as ctx:
         keep = ctx.enter_context(tc.tile_pool(name="keep", bufs=1))
@@ -32,27 +44,20 @@ def tile_relation_trilinear_score_f4_kernel(
 
         scale_bc = keep.tile([128, K], F32, name="scale_bc")
         nc.scalar.dma_start(out=scale_bc[:], in_=x_scale.rearrange("o k -> (o k)").partition_broadcast(128))
-
         warm = keep.tile([128, 1], F32, name="warm")
         nc.vector.memset(warm[:], 0.0)
         nc.scalar.activation(out=warm[:], in_=warm[:], func=ACT.Tanh)
-
         vecs = keep.tile([128, 128], BF16, name="vecs")
         nc.vector.memset(vecs[:], 0.0)
-        nc.scalar.dma_start(out=vecs[0:8, :], in_=b_head.rearrange("(t q) -> t q", q=128))
-        nc.scalar.dma_start(out=vecs[8:16, :], in_=b_tail.rearrange("(t q) -> t q", q=128))
+        for role in range(2):
+            nc.scalar.dma_start(out=vecs[8 * role:8 * role + 8, :], in_=b_in[role].rearrange("(t q) -> t q", q=128))
 
-        x_raw = []
         x_view = x_bytes.rearrange("(g p j) k -> g p j k", p=128, j=4)
-        for g in range(2):
-            xb = keep.tile([128, 4, K], U8, name="x_raw%d" % g)
-            x_raw.append(xb)
+        x_raw = [keep.tile([128, 4, K], U8, name="x_raw%d" % g) for g in range(2)]
+        w_raw, a_raw = {}, {}
 
-        w_raw = {}
-        a_raw = {}
-
-        def load_x(g, j0, j1):
-            nc.sync.dma_start(out=x_raw[g][:, j0:j1, :], in_=x_view[g, :, j0:j1, :])
+        def load_x(g, u):
+            nc.sync.dma_start(out=x_raw[g][:, 2 * u:2 * u + 2, :], in_=x_view[g, :, 2 * u:2 * u + 2, :])
 
         def load_w(role, kk, dh):
             t = work.tile([128, 4, 512], BF16, name="raw", tag="raw", bufs=9, align_bytes=64)
@@ -62,15 +67,15 @@ def tile_relation_trilinear_score_f4_kernel(
 
         def load_a(role, pp):
             t = work.tile([128, 2, T], BF16, name="raw", tag="raw", bufs=9, align_bytes=64)
-            view = a_in[role][pp * 256:(pp + 1) * 256, :]
-            nc.sync.dma_start(out=t[:], in_=view.rearrange("(s p) t -> p s t", p=128))
+            nc.sync.dma_start(out=t[:], in_=a_in[role][pp * 256:(pp + 1) * 256, :].rearrange("(s p) t -> p s t", p=128))
             a_raw[role, pp] = t
 
-        load_x(0, 0, 2)
-        load_x(0, 2, 4)
+        load_x(0, 0)
+        load_x(0, 1)
         load_w(0, 0, 0)
         load_w(0, 1, 0)
-        load_x(1, 0, 4)
+        load_x(1, 0)
+        load_x(1, 1)
         load_w(0, 0, 1)
         load_w(0, 1, 1)
 
@@ -79,243 +84,276 @@ def tile_relation_trilinear_score_f4_kernel(
         ident_bf = keep.tile([128, 128], BF16, name="ident_bf")
         make_identity(nc, ident_bf[:])
 
-        g_sb = []
+        gain = []
         for role in range(2):
-            gain_sb = keep.tile([128, 2, 4], BF16, name="gain_sb%d" % role)
-            nc.scalar.dma_start(out=gain_sb[:], in_=g_in[role].rearrange("(g p j) -> p g j", p=128, j=4))
-            g_sb.append(gain_sb)
+            gt = keep.tile([128, T], BF16, name="gain%d" % role)
+            gain.append(gt)
+        nc.scalar.dma_start(out=gain[0][:], in_=g_in[0].partition_broadcast(128))
         rel_bf = keep.tile([128, C], BF16, name="rel_bf")
         nc.scalar.dma_start(out=rel_bf[:], in_=rel)
         beta_bc = keep.tile([128, R], BF16, name="beta_bc")
         nc.scalar.dma_start(out=beta_bc[:], in_=beta.partition_broadcast(128))
 
-        xq = {}
-        wq = {}
-        aq = {}
-        hq = {}
-        hg = {}
-        xg = {}
-        ag = {}
-        wg = {}
-        th = {}
-        ehs = {}
-        prod = {}
+        rel_f = keep.tile([128, C], F32, name="rel_f")
+        b_t = keep.tile([128, 16], BF16, name="b_t")
 
-        def new_codes(pool, nm):
-            codes = pool.tile([128, 512], U32, name=nm + "_codes", align_bytes=64)
-            scales = pool.tile([128, 512], U8, name=nm + "_scales", align_bytes=64)
-            return codes, scales
+        S = {}
+
+        def codes(nm, width, **kw):
+            c = keep.tile([128, width], U32, name=nm + "_codes", align_bytes=64, **kw)
+            s = keep.tile([128, width], U8, name=nm + "_scales", align_bytes=64, **kw)
+            return c, s
 
         def quantize(dst, src):
             nc.vector.quantize_mx(out=dst[0][:].bitcast(FP8X4), scales=dst[1][:], in_=src)
 
         def mx(acc, lhs, lcols, rhs, start, stop):
             nc.tensor.matmul_mx(
-                out=acc,
-                lhsT=lhs[0][:, lcols].bitcast(FP8X4),
-                lhsT_scale=lhs[1][:, lcols],
-                rhs=rhs[0][:].bitcast(FP8X4),
-                rhs_scale=rhs[1][:],
-                start=start,
-                stop=stop,
+                out=acc, lhsT=lhs[0][:, lcols].bitcast(FP8X4), lhsT_scale=lhs[1][:, lcols],
+                rhs=rhs[0][:].bitcast(FP8X4), rhs_scale=rhs[1][:], start=start, stop=stop,
             )
 
         def copy(eng, out_ap, in_ap):
-            if eng == "s":
+            if eng == "S":
                 nc.scalar.copy(out=out_ap, in_=in_ap)
             else:
                 nc.vector.tensor_copy(out=out_ap, in_=in_ap)
 
-        def x_tile(g, j, eng="s"):
-            xs = work.tile([128, K], BF16, name="xs", tag="xs", bufs=2, align_bytes=64)
-            nc.vector.tensor_tensor(out=xs[:], in0=x_raw[g][:, j, :].bitcast(FP8), in1=scale_bc[:], op=ALU.mult)
-            words = xs[:].bitcast(F32)
+        def xs(g, j):
+            t = work.tile([128, K], BF16, name="xs", tag="xs", bufs=3, align_bytes=64)
+            nc.vector.tensor_tensor(out=t[:], in0=x_raw[g][:, j, :].bitcast(FP8), in1=scale_bc[:], op=ALU.mult)
+            S["xs", g, j] = t
+
+        def xt(g, u, kk):
             bank = psum.tile([128, 2, 2, 128], F32, name="tr", tag="tr", bufs=4)
-            for kk in range(2):
-                for u in range(2):
-                    nc.tensor.transpose(bank[:, kk, u, :], words[:, 256 * kk + u:256 * (kk + 1):2], ident[:])
-            if j == 0:
-                xg[g] = work.tile([128, 2, 512, 4], BF16, name="xg", tag="xg", bufs=1, align_bytes=64)
-            dst = xg[g][:].rearrange("p k n t -> p (k n t)").bitcast(F32)
-            dst = dst.rearrange("p (k n u) -> p k n u", k=2, u=2)[:, :, 128 * j:128 * (j + 1), :]
-            copy(eng, dst, bank[:].rearrange("p k u r -> p k r u"))
+            for e in range(2):
+                words = S["xs", g, 2 * u + e][:].bitcast(F32)
+                for v in range(2):
+                    nc.tensor.transpose(bank[:, e, v, :], words[:, 256 * kk + v:256 * (kk + 1):2], ident[:])
+            S["xt", g, u, kk] = bank
 
-        def x_quant(g, kk):
-            xq[g, kk] = new_codes(keep, "xq%d%d" % (g, kk))
-            quantize(xq[g, kk], xg[g][:, kk].rearrange("p n t -> p (n t)"))
+        def xc(g, u, kk, eng="S"):
+            if u == 0:
+                S["xg", g, kk] = work.tile([128, 512, 4], BF16, name="xg", tag="xg", bufs=2, align_bytes=64)
+            dst = S["xg", g, kk][:].rearrange("p n t -> p (n t)").bitcast(F32)
+            dst = dst.rearrange("p (u q e v) -> p u q e v", u=2, e=2, v=2)[:, u]
+            copy(eng, dst, S["xt", g, u, kk][:].rearrange("p e v q -> p q e v"))
 
-        def w_il(role, kk, dh, eng):
-            t = work.tile([128, 512, 4], BF16, name="grp", tag="grp", bufs=5, align_bytes=64)
-            copy(eng, t[:], w_raw[role, kk, dh][:].rearrange("p j d -> p d j"))
-            wg[role, kk, dh] = t
+        def xq(g, kk):
+            S["xq", g, kk] = codes("xq%d%d" % (g, kk), 512)
+            quantize(S["xq", g, kk], S["xg", g, kk][:].rearrange("p n t -> p (n t)"))
 
-        def w_quant(role, kk, dh):
-            wq[role, kk, dh] = new_codes(keep, "wq%d%d%d" % (role, kk, dh))
-            quantize(wq[role, kk, dh], wg[role, kk, dh][:].rearrange("p d j -> p (d j)"))
+        def wi(role, kk, q, eng):
+            t = work.tile([128, 256, 4], BF16, name="wg", tag="wg", bufs=6, align_bytes=64)
+            src = w_raw[role, kk, q // 2][:, :, 256 * (q % 2):256 * (q % 2 + 1)]
+            copy(eng, t[:], src.rearrange("p j d -> p d j"))
+            S["wi", role, kk, q] = t
 
-        def a_bank(role, g, pp, eng):
+        def wq(role, kk, q):
+            S["wq", role, kk, q] = codes("wq%d%d" % (kk, q), 256, bufs=1)
+            quantize(S["wq", role, kk, q], S["wi", role, kk, q][:].rearrange("p d j -> p (d j)"))
+
+        def at(role, g, pp):
             words = a_raw[role, pp][:].rearrange("p s t -> p (s t)").bitcast(F32)
             bank = psum.tile([128, 2, 2, 128], F32, name="tr", tag="tr", bufs=4)
             for s in range(2):
                 for u in range(2):
                     w0 = 512 * s + 256 * g
                     nc.tensor.transpose(bank[:, s, u, :], words[:, w0 + u:w0 + 256:2], ident[:])
-            ph = pp // 2
-            if (role, g, ph) not in ag:
-                ag[role, g, ph] = work.tile([128, 512, 4], BF16, name="grp", tag="grp", bufs=5, align_bytes=64)
-            dst = ag[role, g, ph][:].rearrange("p n t -> p (n t)").bitcast(F32)
+            S["at", role, g, pp] = bank
+
+        def ac(role, g, pp, eng):
+            if pp % 2 == 0:
+                S["ag", role, g, pp // 2] = work.tile([128, 512, 4], BF16, name="ag", tag="ag", bufs=4, align_bytes=64)
+            dst = S["ag", role, g, pp // 2][:].rearrange("p n t -> p (n t)").bitcast(F32)
             dst = dst.rearrange("p (s r u) -> p s r u", s=4, u=2)[:, 2 * (pp % 2):2 * (pp % 2) + 2]
-            copy(eng, dst, bank[:].rearrange("p s u r -> p s r u"))
+            copy(eng, dst, S["at", role, g, pp][:].rearrange("p s u r -> p s r u"))
 
-        def a_quant(role, g, ph):
-            aq[role, g, ph] = new_codes(keep, "aq%d%d%d" % (role, g, ph))
-            quantize(aq[role, g, ph], ag[role, g, ph][:].rearrange("p n t -> p (n t)"))
+        def aq(role, g, ph):
+            S["aq", role, g, ph] = codes("aq%d%d%d" % (role, g, ph), 512)
+            quantize(S["aq", role, g, ph], S["ag", role, g, ph][:].rearrange("p n t -> p (n t)"))
 
-        def unit_mm(role, g, dt):
+        def mm(role, g, dt):
             acc = psum.tile([128, 512], F32, name="mm", tag="mm", bufs=4)
-            cols = slice(128 * (dt % 4), 128 * (dt % 4 + 1))
+            cols = slice(128 * (dt % 2), 128 * (dt % 2 + 1))
             for kk in range(2):
-                mx(acc[:], wq[role, kk, dt // 4], cols, xq[g, kk], kk == 0, kk == 1)
-            t = work.tile([128, 512], F32, name="th", tag="th", bufs=4)
-            nc.scalar.activation(out=t[:], in_=acc[:], func=ACT.Tanh, bias=b_t[:, 8 * role + dt:8 * role + dt + 1])
-            th[role, g, dt] = t
+                mx(acc[:], S["wq", role, kk, dt // 2], cols, S["xq", g, kk], kk == 0, kk == 1)
+            S["mm", role, g, dt] = acc
 
-        def unit_tr(role, g, dt):
-            t = th[role, g, dt]
-            bank = psum.tile([128, 4, 128], F32, name="tr", tag="tr", bufs=4)
-            for j in range(4):
-                nc.tensor.transpose(bank[:, j, :], t[:, 128 * j:128 * (j + 1)], ident[:])
-            if dt == 0:
-                hg[role, g] = work.tile([128, C, 128, 4], BF16, name="hg", tag="hg", bufs=2, align_bytes=64)
-            gain = g_sb[role][:, g, :].unsqueeze(1).unsqueeze(1).to_broadcast([128, C, 16, 4])
+        def th(role, g, dt):
+            t = work.tile([128, 512], F32, name="th", tag="th", bufs=4)
+            col = 8 * role + dt
+            nc.scalar.activation(out=t[:], in_=S["mm", role, g, dt][:], func=ACT.Tanh, bias=b_t[:, col:col + 1])
+            S["th", role, g, dt] = t
+
+        def gm(role, g, dt):
+            t = work.tile([128, 512], BF16, name="gm", tag="gm", bufs=6, align_bytes=64)
             nc.vector.tensor_tensor(
-                out=hg[role, g][:, :, 16 * dt:16 * (dt + 1), :],
-                in0=bank[:].rearrange("p j (r c) -> p c r j", c=C),
-                in1=gain,
+                out=t[:].rearrange("p (u q e) -> p u q e", u=2, e=2),
+                in0=S["th", role, g, dt][:].rearrange("p (u q e) -> p u q e", u=2, e=2),
+                in1=gain[role][:, 512 * g:512 * (g + 1)].rearrange("p (q u e) -> p u q e", u=2, e=2),
                 op=ALU.mult,
             )
+            S["gm", role, g, dt] = t
 
-        def h_quant(role, g, ch):
-            hq[role, g, ch] = new_codes(keep, "hq%d%d%d" % (role, g, ch))
-            quantize(hq[role, g, ch], hg[role, g][:, 4 * ch:4 * ch + 4].rearrange("p c r t -> p (c r t)"))
+        def ht(role, g, dt):
+            bank = psum.tile([128, 2, 256], F32, name="tr", tag="tr", bufs=4)
+            for s in range(2):
+                words = S["gm", role, g, dt + s][:].bitcast(F32)
+                for u in range(2):
+                    nc.tensor.transpose(bank[:, u, 128 * s:128 * (s + 1)], words[:, 128 * u:128 * (u + 1)], ident[:])
+            S["ht", role, g, dt] = bank
 
-        def pooled(role, c, ph):
+        def tt(role, g, dt, eng):
+            if dt == 0:
+                S["hg", role, g] = work.tile([128, C, 128, 4], BF16, name="hg", tag="hg", bufs=2, align_bytes=64)
+            dst = S["hg", role, g][:].rearrange("p c r t -> p (c r t)").bitcast(F32)
+            dst = dst.rearrange("p (c r u) -> p c r u", c=C, u=2)[:, :, 16 * dt:16 * dt + 32, :]
+            copy(eng, dst, S["ht", role, g, dt][:].rearrange("p u (r c) -> p c r u", c=C))
+
+        def hq(role, g, ch):
+            S["hq", role, g, ch] = codes("hq%d%d%d" % (role, g, ch), 512)
+            quantize(S["hq", role, g, ch], S["hg", role, g][:, 4 * ch:4 * ch + 4].rearrange("p c r t -> p (c r t)"))
+
+        def pm(role, c, ph):
             acc = psum.tile([128, 512], F32, name="mm", tag="mm", bufs=4)
             cols = slice(128 * (c % 4), 128 * (c % 4 + 1))
             for g in range(2):
-                mx(acc[:], hq[role, g, c // 4], cols, aq[role, g, ph], g == 0, g == 1)
-            return acc
+                mx(acc[:], S["hq", role, g, c // 4], cols, S["aq", role, g, ph], g == 0, g == 1)
+            S["pm", role, c, ph] = acc
 
-        def eh(c, ph):
-            acc = pooled(0, c, ph)
+        def es(c, ph):
             t = work.tile([128, 512], F32, name="ehs", tag="ehs", bufs=16)
-            nc.scalar.activation(out=t[:], in_=acc[:], func=ACT.Copy, scale=rel_f[:, c:c + 1])
-            ehs[c, ph] = t
+            nc.scalar.activation(out=t[:], in_=S["pm", 0, c, ph][:], func=ACT.Copy, scale=rel_f[:, c:c + 1])
+            S["es", c, ph] = t
 
-        def et(c, ph):
-            acc = pooled(1, c, ph)
-            t = work.tile([128, 512], F32, name="prod", tag="prod", bufs=5)
-            nc.vector.tensor_tensor(out=t[:], in0=acc[:], in1=ehs[c, ph][:], op=ALU.mult)
-            prod[c, ph] = t
+        def ev(c, ph):
+            t = work.tile([128, 512], F32, name="prod", tag="prod", bufs=8)
+            nc.vector.tensor_tensor(out=t[:], in0=S["pm", 1, c, ph][:], in1=S["es", c, ph][:], op=ALU.mult)
+            S["ev", c, ph] = t
 
-        score = {}
-
-        def sum_tr(c, ph):
+        def st(c, ph):
             for m in range(4):
                 if c == 0:
-                    score[ph, m] = psum.tile([128, 128], F32, name="tr", tag="tr", bufs=4)
+                    S["sum", ph, m] = psum.tile([128, 128], F32, name="tr", tag="tr", bufs=4)
                 nc.tensor.matmul(
-                    score[ph, m][:],
-                    lhsT=prod[c, ph][:, 128 * m:128 * (m + 1)],
-                    rhs=ident[:],
-                    is_transpose=True,
-                    start=(c == 0),
-                    stop=(c == C - 1),
+                    S["sum", ph, m][:], lhsT=S["ev", c, ph][:, 128 * m:128 * (m + 1)], rhs=ident[:],
+                    is_transpose=True, start=(c == 0), stop=(c == C - 1),
                 )
 
-        def finish(ph):
+        def fin(ph):
             o = work.tile([128, 4, R], F32, name="o", tag="o", bufs=2)
             for m in range(4):
-                nc.vector.tensor_tensor(out=o[:, m, :], in0=score[ph, m][:], in1=beta_bc[:], op=ALU.add)
+                nc.vector.tensor_tensor(out=o[:, m, :], in0=S["sum", ph, m][:], in1=beta_bc[:], op=ALU.add)
             nc.sync.dma_start(out=out[512 * ph:512 * (ph + 1), :].rearrange("(m p) r -> p m r", p=128), in_=o[:])
-
-        rel_f = keep.tile([128, C], F32, name="rel_f")
-        nc.vector.tensor_copy(out=rel_f[:], in_=rel_bf[:])
-        b_ps = psum.tile([128, 128], BF16, name="tr", tag="tr", bufs=4)
-        nc.tensor.transpose(b_ps[:], vecs[:], ident_bf[:])
-        b_t = keep.tile([128, 16], BF16, name="b_t")
-        nc.vector.tensor_copy(out=b_t[:], in_=b_ps[:, 0:16])
-
-        for j in range(4):
-            x_tile(0, j)
-        w_il(0, 0, 0, "s")
-        w_il(0, 1, 0, "v")
-        x_quant(0, 0)
-        x_quant(0, 1)
-        w_quant(0, 0, 0)
-        w_quant(0, 1, 0)
 
         for pp in range(4):
             load_a(0, pp)
+        nc.sync.dma_start(out=gain[1][:], in_=g_in[1].partition_broadcast(128))
         for dh in range(2):
             for kk in range(2):
                 load_w(1, kk, dh)
         for pp in range(4):
             load_a(1, pp)
 
+        ctx.enter_context(tc.manual_schedule())
+        b_ps = psum.tile([128, 128], BF16, name="tr", tag="tr", bufs=4)
+        nc.tensor.transpose(b_ps[:], vecs[:], ident_bf[:])
+        xs(0, 0)
+        xs(0, 1)
+        nc.vector.tensor_copy(out=b_t[:], in_=b_ps[:, 0:16])
+        xs(0, 2)
+        xs(0, 3)
+        nc.vector.tensor_copy(out=rel_f[:], in_=rel_bf[:])
+        wi(0, 0, 0, "S")
+        wi(0, 1, 0, "S")
+        for u in range(2):
+            for kk in range(2):
+                xt(0, u, kk)
+                xc(0, u, kk)
+        wq(0, 0, 0)
+        wq(0, 1, 0)
+        for j in range(X_PRE):
+            xs(1, j)
+        xq(0, 0)
+        xq(0, 1)
+        wi(0, 0, 1, "S")
+        wi(0, 1, 1, "S")
+        wq(0, 0, 1)
+        wq(0, 1, 1)
+        for j in range(X_PRE, 4):
+            xs(1, j)
         groups = [(role, g, dt) for role in range(2) for g in range(2) for dt in range(0, 8, 2)]
-        for i in range(len(groups) + 1):
-            if i < len(groups):
+        banks = [(role, g, pp) for role in range(2) for pp in range(4) for g in range(2)]
+        halves = [(ph, c) for ph in range(2) for c in range(C)]
+        a_ready = {}
+        for i in range(18):
+            if i < 16:
                 role, g, dt = groups[i]
-                unit_mm(role, g, dt)
-                unit_mm(role, g, dt + 1)
-            if i > 0:
+                for d in (dt, dt + 1):
+                    mm(role, g, d)
+                for d in (dt, dt + 1):
+                    th(role, g, d)
+            mine = [halves[n] for n in range(16) if EH_SLOT[n] == i]
+            for ph, c in mine:
+                pm(0, c, ph)
+            for ph, c in mine:
+                es(c, ph)
+            if i in (X1_SLOT, X1_SLOT + 1):
+                for kk in range(2):
+                    xt(1, i - X1_SLOT, kk)
+                for kk in range(2):
+                    xc(1, i - X1_SLOT, kk)
+            if 1 <= i <= 16:
                 role, g, dt = groups[i - 1]
-                unit_tr(role, g, dt)
-                unit_tr(role, g, dt + 1)
-                if dt == 6:
-                    h_quant(role, g, 0)
-                    h_quant(role, g, 1)
-            if i == 0:
-                x_tile(1, 0)
-                x_tile(1, 1)
-                w_il(0, 0, 1, "s")
-                w_il(0, 1, 1, "s")
-            if i == 1:
-                w_quant(0, 0, 1)
-                w_quant(0, 1, 1)
-                x_tile(1, 2)
-                x_tile(1, 3)
-            if i == 2:
-                x_quant(1, 0)
-                x_quant(1, 1)
-            if 4 <= i < 8:
-                pp = i - 4
-                a_bank(0, 0, pp, "s")
-                a_bank(0, 1, pp, "s")
-                if pp % 2 == 1:
-                    a_quant(0, 0, pp // 2)
-                    a_quant(0, 1, pp // 2)
-            if 4 <= i < 8:
-                kk, dh = i % 2, (i - 4) // 2
-                w_il(1, kk, dh, "v" if kk else "s")
-                w_quant(1, kk, dh)
-            if 8 <= i < 16:
-                pp, g = (i - 8) // 2, i % 2
-                a_bank(1, g, pp, "v")
-                if pp % 2 == 1:
-                    a_quant(1, g, pp // 2)
-            if 10 <= i:
-                first = 2 * (i - 10)
-                for n in range(first, first + (2 if i < 16 else 4)):
-                    eh(n % 8, n // 8)
-
-        pairs = [(ph, c) for ph in range(2) for c in range(C)]
-        for n in range(len(pairs) + 2):
-            if n < len(pairs):
-                et(pairs[n][1], pairs[n][0])
-            if n >= 2:
-                ph, c = pairs[n - 2]
-                sum_tr(c, ph)
+                for d in (dt, dt + 1):
+                    gm(role, g, d)
+            if i >= 2:
+                role, g, dt = groups[i - 2]
+                ht(role, g, dt)
+                tt(role, g, dt, TT_ENG[i])
+            for n in range(16):
+                if AT_SLOT[n] == i:
+                    at(*banks[n])
+                    ac(*banks[n], AC_ENG[n])
+                    a_ready[banks[n]] = i
+            for q in range(4):
+                for role in range(2):
+                    slot = W_SLOT[role][q]
+                    if slot == i:
+                        wi(role, 0, q, W_ENG[role][0])
+                        wi(role, 1, q, W_ENG[role][1])
+                    if slot is not None and slot + 1 == i:
+                        wq(role, 0, q)
+                        wq(role, 1, q)
+            if i == X1_SLOT + 2:
+                xq(1, 0)
+                xq(1, 1)
+            if i >= 2 and dt_of(groups, i - 2) == 6:
+                role, g, dt = groups[i - 2]
+                for ch in range(2):
+                    hq(role, g, ch)
+            for role in range(2):
+                for half in range(2):
+                    for g in range(2):
+                        last = max(AT_SLOT[8 * role + 2 * pp + g] for pp in (2 * half, 2 * half + 1))
+                        if min(17, last + AQ_LAG) == i:
+                            aq(role, g, half)
+        done = 0
+        before = []
+        for n in SUM_RUNS + (0,):
+            now = halves[done:done + n]
+            done += n
+            for ph, c in now:
+                pm(1, c, ph)
+            for ph, c in now:
+                ev(c, ph)
+            for ph, c in before:
+                st(c, ph)
                 if c == C - 1:
-                    finish(ph)
+                    fin(ph)
+            before = now
+
+
+def dt_of(groups, i):
+    return groups[i][2]

@@ -16,15 +16,22 @@ FP8X4 = mybir.dt.float8_e4m3fn_x4
 ACT = mybir.ActivationFunctionType
 ALU = mybir.AluOpType
 
-X_PRE = 2
-X1_SLOT = 0
-EH_SLOT = (11, 11, 11, 11, 11, 12, 13, 14, 14, 14, 15, 15, 15, 17, 17, 17)
-TT_ENG = "SSSVSSSSSVVVSSSSSV"
-AT_SLOT = (0, 1, 1, 3, 5, 8, 9, 10, 3, 5, 5, 7, 7, 10, 14, 15)
-AC_ENG = "VSSVSSVVVSSVSVSS"
-W_SLOT = ((None, None, 0, 0), (3, 5, 7, 8))
-W_ENG = ("SV", "VS")
-AQ_LAG = 2
+X1_SLOT = (-1, 0)
+XQ_LAG = 0
+Q0_ENG = "S"
+GAIN_LATE = 1
+SWAP = 1
+GP_SLOT = 3
+W_ON_TENSOR = ()
+EH_COUNT = (0, 0, 0, 0, 0, 0, 5, 7, 4)
+TT_ENG = "VSSSSVSSSSVVVSSSSV"
+AT_SLOT = (0, 0, 0, 0, 0, 3, 3, 3, 3, 3, 4, 4, 5, 5, 6, 6)
+AT_FIRST = 2
+AC_ENG = "SSSSSSSSSSVSVVSV"
+W_SLOT = (-1, -1, 0, 0, 2, 1, 0, 3)
+W_ENG = "SSSVSVSVVVVVVSVS"
+WQ_LAG = 0
+AQ_LAG = 1
 SUM_RUNS = (4, 4, 4, 4)
 
 
@@ -42,8 +49,12 @@ def tile_relation_trilinear_score_f4_kernel(
         work = ctx.enter_context(tc.tile_pool(name="work", bufs=2))
         psum = ctx.enter_context(tc.psum_pool(name="psum", bufs=4))
 
-        scale_bc = keep.tile([128, K], F32, name="scale_bc")
-        nc.scalar.dma_start(out=scale_bc[:], in_=x_scale.rearrange("o k -> (o k)").partition_broadcast(128))
+        scale_raw = keep.tile([128, 2, 4], F32, name="scale_raw")
+        nc.scalar.dma_start(out=scale_raw[:], in_=x_scale.rearrange("o (k p t) -> p (o k) t", k=2, p=128))
+        gain_rows = keep.tile([128, T], BF16, name="gain_rows")
+        nc.vector.memset(gain_rows[:], 0.0)
+        for role in range(2):
+            nc.scalar.dma_start(out=gain_rows[role:role + 1, :], in_=g_in[role].rearrange("(o t) -> o t", o=1))
         warm = keep.tile([128, 1], F32, name="warm")
         nc.vector.memset(warm[:], 0.0)
         nc.scalar.activation(out=warm[:], in_=warm[:], func=ACT.Tanh)
@@ -84,15 +95,10 @@ def tile_relation_trilinear_score_f4_kernel(
         ident_bf = keep.tile([128, 128], BF16, name="ident_bf")
         make_identity(nc, ident_bf[:])
 
-        gain = []
-        for role in range(2):
-            gt = keep.tile([128, T], BF16, name="gain%d" % role)
-            gain.append(gt)
-        nc.scalar.dma_start(out=gain[0][:], in_=g_in[0].partition_broadcast(128))
         rel_bf = keep.tile([128, C], BF16, name="rel_bf")
         nc.scalar.dma_start(out=rel_bf[:], in_=rel)
         beta_bc = keep.tile([128, R], BF16, name="beta_bc")
-        nc.scalar.dma_start(out=beta_bc[:], in_=beta.partition_broadcast(128))
+        scale8 = keep.tile([128, 2, 2, 4], F32, name="scale8")
 
         rel_f = keep.tile([128, C], F32, name="rel_f")
         b_t = keep.tile([128, 16], BF16, name="b_t")
@@ -119,38 +125,77 @@ def tile_relation_trilinear_score_f4_kernel(
             else:
                 nc.vector.tensor_copy(out=out_ap, in_=in_ap)
 
-        def xs(g, j):
-            t = work.tile([128, K], BF16, name="xs", tag="xs", bufs=3, align_bytes=64)
-            nc.vector.tensor_tensor(out=t[:], in0=x_raw[g][:, j, :].bitcast(FP8), in1=scale_bc[:], op=ALU.mult)
-            S["xs", g, j] = t
+        def wd(g, u, eng):
+            t = work.tile([128, 2, K], BF16, name="xw", tag="big", bufs=8, align_bytes=64)
+            copy(eng, t[:].rearrange("p e k -> p (e k)"), x_raw[g][:, 2 * u:2 * u + 2, :].rearrange("p e k -> p (e k)").bitcast(FP8))
+            S["wd", g, u] = t
 
         def xt(g, u, kk):
             bank = psum.tile([128, 2, 2, 128], F32, name="tr", tag="tr", bufs=4)
             for e in range(2):
-                words = S["xs", g, 2 * u + e][:].bitcast(F32)
+                words = S["wd", g, u][:, e, :].bitcast(F32)
                 for v in range(2):
                     nc.tensor.transpose(bank[:, e, v, :], words[:, 256 * kk + v:256 * (kk + 1):2], ident[:])
             S["xt", g, u, kk] = bank
 
-        def xc(g, u, kk, eng="S"):
+        def xs(g, u, kk):
             if u == 0:
-                S["xg", g, kk] = work.tile([128, 512, 4], BF16, name="xg", tag="xg", bufs=2, align_bytes=64)
-            dst = S["xg", g, kk][:].rearrange("p n t -> p (n t)").bitcast(F32)
-            dst = dst.rearrange("p (u q e v) -> p u q e v", u=2, e=2, v=2)[:, u]
-            copy(eng, dst, S["xt", g, u, kk][:].rearrange("p e v q -> p q e v"))
+                S["xg", g, kk] = work.tile([128, 2, 1024], BF16, name="xg", tag="big", bufs=8, align_bytes=64)
+            nc.vector.tensor_tensor(
+                out=S["xg", g, kk][:, u, :].rearrange("p (q w b) -> p q w b", w=4, b=2),
+                in0=S["xt", g, u, kk][:].rearrange("p e v q -> p (e v q)").bitcast(BF16).rearrange("p (w q b) -> p q w b", w=4, b=2),
+                in1=scale8[:, kk].rearrange("p e t -> p (e t)").rearrange("p (w b) -> p w b", b=2).unsqueeze(1).to_broadcast([128, 128, 4, 2]),
+                op=ALU.mult,
+            )
+
+        def gp(role, g):
+            bank = psum.tile([128, 512], F32, name="tr", tag="tr", bufs=4)
+            nc.tensor.matmul(
+                bank[:], lhsT=ident_bf[:, role:role + 1].to_broadcast([128, 128]),
+                rhs=gain_rows[:, 512 * g:512 * (g + 1)], start=True, stop=True,
+            )
+            S["gp", role, g] = bank
+
+        def gb(role, g):
+            t = keep.tile([128, 512], BF16, name="gain%d%d" % (role, g), align_bytes=64)
+            nc.scalar.copy(
+                out=t[:].rearrange("p (u q e) -> p u q e", u=2, e=2),
+                in_=S["gp", role, g][:].rearrange("p (q u e) -> p u q e", u=2, e=2),
+            )
+            S["gain", role, g] = t
+
+        def x1(u):
+            for kk in range(2):
+                xt(1, u, kk)
+            for kk in range(2):
+                xs(1, u, kk)
+
+        def wt(role, kk, q):
+            bank = psum.tile([128, 1024], BF16, name="tr", tag="tr", bufs=4)
+            for h in range(2):
+                d0 = 256 * (q % 2) + 128 * h
+                nc.tensor.matmul(
+                    bank[:, 512 * h:512 * (h + 1)], lhsT=ident_bf[:],
+                    rhs=w_raw[role, kk, q // 2][:, :, d0:d0 + 128].rearrange("p j d -> p d j"), start=True, stop=True,
+                )
+            S["wt", role, kk, q] = bank
 
         def xq(g, kk):
             S["xq", g, kk] = codes("xq%d%d" % (g, kk), 512)
-            quantize(S["xq", g, kk], S["xg", g, kk][:].rearrange("p n t -> p (n t)"))
+            quantize(S["xq", g, kk], S["xg", g, kk][:].rearrange("p u n -> p (u n)"))
 
         def wi(role, kk, q, eng):
             t = work.tile([128, 256, 4], BF16, name="wg", tag="wg", bufs=6, align_bytes=64)
-            src = w_raw[role, kk, q // 2][:, :, 256 * (q % 2):256 * (q % 2 + 1)]
-            copy(eng, t[:], src.rearrange("p j d -> p d j"))
+            if role == 0 and q in W_ON_TENSOR:
+                wt(role, kk, q)
+                copy(eng, t[:].rearrange("p d j -> p (d j)"), S["wt", role, kk, q][:])
+            else:
+                src = w_raw[role, kk, q // 2][:, :, 256 * (q % 2):256 * (q % 2 + 1)]
+                copy(eng, t[:], src.rearrange("p j d -> p d j"))
             S["wi", role, kk, q] = t
 
         def wq(role, kk, q):
-            S["wq", role, kk, q] = codes("wq%d%d" % (kk, q), 256, bufs=1)
+            S["wq", role, kk, q] = codes("wq%d%d" % (kk, q), 256, bufs=2)
             quantize(S["wq", role, kk, q], S["wi", role, kk, q][:].rearrange("p d j -> p (d j)"))
 
         def at(role, g, pp):
@@ -181,19 +226,14 @@ def tile_relation_trilinear_score_f4_kernel(
             S["mm", role, g, dt] = acc
 
         def th(role, g, dt):
-            t = work.tile([128, 512], F32, name="th", tag="th", bufs=4)
+            t = work.tile([128, 512], F32, name="th", tag="th", bufs=6)
             col = 8 * role + dt
             nc.scalar.activation(out=t[:], in_=S["mm", role, g, dt][:], func=ACT.Tanh, bias=b_t[:, col:col + 1])
             S["th", role, g, dt] = t
 
         def gm(role, g, dt):
             t = work.tile([128, 512], BF16, name="gm", tag="gm", bufs=6, align_bytes=64)
-            nc.vector.tensor_tensor(
-                out=t[:].rearrange("p (u q e) -> p u q e", u=2, e=2),
-                in0=S["th", role, g, dt][:].rearrange("p (u q e) -> p u q e", u=2, e=2),
-                in1=gain[role][:, 512 * g:512 * (g + 1)].rearrange("p (q u e) -> p u q e", u=2, e=2),
-                op=ALU.mult,
-            )
+            nc.vector.tensor_tensor(out=t[:], in0=S["th", role, g, dt][:], in1=S["gain", role, g][:], op=ALU.mult)
             S["gm", role, g, dt] = t
 
         def ht(role, g, dt):
@@ -223,13 +263,14 @@ def tile_relation_trilinear_score_f4_kernel(
             S["pm", role, c, ph] = acc
 
         def es(c, ph):
-            t = work.tile([128, 512], F32, name="ehs", tag="ehs", bufs=16)
-            nc.scalar.activation(out=t[:], in_=S["pm", 0, c, ph][:], func=ACT.Copy, scale=rel_f[:, c:c + 1])
-            S["es", c, ph] = t
+            if ph == 0:
+                S["ehs", c] = work.tile([128, 2, 512], F32, name="ehs", tag="big", bufs=8, align_bytes=64)
+            S["es", c, ph] = S["ehs", c][:, ph, :]
+            nc.scalar.activation(out=S["es", c, ph], in_=S["pm", 0, c, ph][:], func=ACT.Copy, scale=rel_f[:, c:c + 1])
 
         def ev(c, ph):
             t = work.tile([128, 512], F32, name="prod", tag="prod", bufs=8)
-            nc.vector.tensor_tensor(out=t[:], in0=S["pm", 1, c, ph][:], in1=S["es", c, ph][:], op=ALU.mult)
+            nc.vector.tensor_tensor(out=t[:], in0=S["pm", 1, c, ph][:], in1=S["es", c, ph], op=ALU.mult)
             S["ev", c, ph] = t
 
         def st(c, ph):
@@ -242,14 +283,14 @@ def tile_relation_trilinear_score_f4_kernel(
                 )
 
         def fin(ph):
-            o = work.tile([128, 4, R], F32, name="o", tag="o", bufs=2)
+            o = work.tile([128, 4, R], F32, name="o", tag="o", bufs=1)
             for m in range(4):
                 nc.vector.tensor_tensor(out=o[:, m, :], in0=S["sum", ph, m][:], in1=beta_bc[:], op=ALU.add)
             nc.sync.dma_start(out=out[512 * ph:512 * (ph + 1), :].rearrange("(m p) r -> p m r", p=128), in_=o[:])
 
         for pp in range(4):
             load_a(0, pp)
-        nc.sync.dma_start(out=gain[1][:], in_=g_in[1].partition_broadcast(128))
+        nc.sync.dma_start(out=beta_bc[:], in_=beta.partition_broadcast(128))
         for dh in range(2):
             for kk in range(2):
                 load_w(1, kk, dh)
@@ -257,88 +298,117 @@ def tile_relation_trilinear_score_f4_kernel(
             load_a(1, pp)
 
         ctx.enter_context(tc.manual_schedule())
+        wd(0, 0, "V")
+        wd(0, 1, "S")
         b_ps = psum.tile([128, 128], BF16, name="tr", tag="tr", bufs=4)
         nc.tensor.transpose(b_ps[:], vecs[:], ident_bf[:])
-        xs(0, 0)
-        xs(0, 1)
-        nc.vector.tensor_copy(out=b_t[:], in_=b_ps[:, 0:16])
-        xs(0, 2)
-        xs(0, 3)
-        nc.vector.tensor_copy(out=rel_f[:], in_=rel_bf[:])
-        wi(0, 0, 0, "S")
-        wi(0, 1, 0, "S")
-        for u in range(2):
-            for kk in range(2):
+        nc.vector.tensor_copy(out=scale8[:], in_=scale_raw[:].unsqueeze(2).to_broadcast([128, 2, 2, 4]))
+        for kk in range(2):
+            for u in range(2):
                 xt(0, u, kk)
-                xc(0, u, kk)
+        nc.vector.tensor_copy(out=b_t[:], in_=b_ps[:, 0:16])
+        wi(0, 0, 0, "S")
+        wi(0, 1, 0, Q0_ENG)
+        if not GAIN_LATE:
+            gp(0, 0)
+            gb(0, 0)
+        xs(0, 0, 0)
+        xs(0, 1, 0)
+        xq(0, 0)
         wq(0, 0, 0)
         wq(0, 1, 0)
-        for j in range(X_PRE):
-            xs(1, j)
-        xq(0, 0)
-        xq(0, 1)
+        if SWAP:
+            wd(1, 0, "S")
         wi(0, 0, 1, "S")
         wi(0, 1, 1, "S")
+        xs(0, 0, 1)
+        xs(0, 1, 1)
+        xq(0, 1)
         wq(0, 0, 1)
         wq(0, 1, 1)
-        for j in range(X_PRE, 4):
-            xs(1, j)
-        groups = [(role, g, dt) for role in range(2) for g in range(2) for dt in range(0, 8, 2)]
+        if not SWAP:
+            wd(1, 0, "S")
+        wd(1, 1, "S")
+        for u in range(2):
+            if X1_SLOT[u] < 0:
+                x1(u)
+        if GAIN_LATE:
+            gp(0, 0)
+            gb(0, 0)
+        gp(0, 1)
+        gb(0, 1)
+        nc.vector.tensor_copy(out=rel_f[:], in_=rel_bf[:])
+        quads = [(role, g, half) for role in range(2) for g in range(2) for half in range(2)]
         banks = [(role, g, pp) for role in range(2) for pp in range(4) for g in range(2)]
         halves = [(ph, c) for ph in range(2) for c in range(C)]
-        a_ready = {}
-        for i in range(18):
-            if i < 16:
-                role, g, dt = groups[i]
-                for d in (dt, dt + 1):
-                    mm(role, g, d)
-                for d in (dt, dt + 1):
-                    th(role, g, d)
-            mine = [halves[n] for n in range(16) if EH_SLOT[n] == i]
-            for ph, c in mine:
-                pm(0, c, ph)
-            for ph, c in mine:
-                es(c, ph)
-            if i in (X1_SLOT, X1_SLOT + 1):
-                for kk in range(2):
-                    xt(1, i - X1_SLOT, kk)
-                for kk in range(2):
-                    xc(1, i - X1_SLOT, kk)
-            if 1 <= i <= 16:
-                role, g, dt = groups[i - 1]
-                for d in (dt, dt + 1):
-                    gm(role, g, d)
-            if i >= 2:
-                role, g, dt = groups[i - 2]
-                ht(role, g, dt)
-                tt(role, g, dt, TT_ENG[i])
-            for n in range(16):
-                if AT_SLOT[n] == i:
-                    at(*banks[n])
-                    ac(*banks[n], AC_ENG[n])
-                    a_ready[banks[n]] = i
-            for q in range(4):
-                for role in range(2):
-                    slot = W_SLOT[role][q]
-                    if slot == i:
-                        wi(role, 0, q, W_ENG[role][0])
-                        wi(role, 1, q, W_ENG[role][1])
-                    if slot is not None and slot + 1 == i:
-                        wq(role, 0, q)
-                        wq(role, 1, q)
-            if i == X1_SLOT + 2:
+
+        def a_run(run):
+            for n in run:
+                at(*banks[n])
+            for n in run:
+                ac(*banks[n], AC_ENG[n])
+
+        first = 0
+        for i in range(9):
+            mine = halves[first:first + EH_COUNT[i]]
+            first += EH_COUNT[i]
+
+            def eh_run():
+                for ph, c in mine:
+                    pm(0, c, ph)
+                for ph, c in mine:
+                    es(c, ph)
+
+            if i < 8:
+                role, g, half = quads[i]
+                for dt in range(4 * half, 4 * half + 4):
+                    mm(role, g, dt)
+                for dt in range(4 * half, 4 * half + 4):
+                    th(role, g, dt)
+                eh_run()
+            if i == GP_SLOT:
+                for g in range(2):
+                    gp(1, g)
+                    gb(1, g)
+            for u in range(2):
+                if X1_SLOT[u] == i:
+                    x1(u)
+            run = [n for n in range(16) if AT_SLOT[n] == i]
+            a_run(run[:AT_FIRST])
+            if i >= 1:
+                role, g, half = quads[i - 1]
+                for dt in (4 * half, 4 * half + 2):
+                    ht(role, g, dt)
+                for n, dt in enumerate((4 * half, 4 * half + 2)):
+                    tt(role, g, dt, TT_ENG[2 * i + n])
+            if i == 8:
+                eh_run()
+            if i == max(0, max(X1_SLOT) + XQ_LAG):
                 xq(1, 0)
                 xq(1, 1)
-            if i >= 2 and dt_of(groups, i - 2) == 6:
-                role, g, dt = groups[i - 2]
+            if i < 8:
+                role, g, half = quads[i]
+                for dt in range(4 * half, 4 * half + 4):
+                    gm(role, g, dt)
+            a_run(run[AT_FIRST:])
+            for role in range(2):
+                for q in range(4):
+                    if W_SLOT[4 * role + q] == i:
+                        for kk in range(2):
+                            wi(role, kk, q, W_ENG[8 * role + 2 * q + kk])
+                    if W_SLOT[4 * role + q] >= 0 and W_SLOT[4 * role + q] + WQ_LAG == i:
+                        for kk in range(2):
+                            wq(role, kk, q)
+            if i >= 1 and quads[i - 1][2] == 1:
+                role, g, half = quads[i - 1]
                 for ch in range(2):
                     hq(role, g, ch)
             for role in range(2):
-                for half in range(2):
+                for ph in range(2):
                     for g in range(2):
-                        last = max(AT_SLOT[8 * role + 2 * pp + g] for pp in (2 * half, 2 * half + 1))
-                        if min(17, last + AQ_LAG) == i:
-                            aq(role, g, half)
+                        last = max(AT_SLOT[8 * role + 2 * pp + g] for pp in (2 * ph, 2 * ph + 1))
+                        if last + AQ_LAG == i:
+                            aq(role, g, ph)
         done = 0
         before = []
         for n in SUM_RUNS + (0,):
@@ -353,7 +423,3 @@ def tile_relation_trilinear_score_f4_kernel(
                 if c == C - 1:
                     fin(ph)
             before = now
-
-
-def dt_of(groups, i):
-    return groups[i][2]

@@ -16,23 +16,25 @@ FP8X4 = mybir.dt.float8_e4m3fn_x4
 ACT = mybir.ActivationFunctionType
 ALU = mybir.AluOpType
 
-X1_SLOT = (-1, 0)
+X1_SLOT = (-1, -1)
 XQ_LAG = 0
 Q0_ENG = "S"
-GAIN_LATE = 1
+Q1_ENG = "V"
 SWAP = 1
-GP_SLOT = 3
-W_ON_TENSOR = ()
-EH_COUNT = (0, 0, 0, 0, 0, 0, 5, 7, 4)
-TT_ENG = "VSSSSVSSSSVVVSSSSV"
-AT_SLOT = (0, 0, 0, 0, 0, 3, 3, 3, 3, 3, 4, 4, 5, 5, 6, 6)
-AT_FIRST = 2
-AC_ENG = "SSSSSSSSSSVSVVSV"
-W_SLOT = (-1, -1, 0, 0, 2, 1, 0, 3)
-W_ENG = "SSSVSVSVVVVVVSVS"
+GP_SLOT = 0
+DM = (5, 1, 0, 4, 3, 0, 0, 0, 0, 0, 0, 0, 0, 0, 0, 0, 0, 0)
+EH_COUNT = (0, 0, 0, 0, 0, 0, 4, 8, 4)
+HT_LATE = (1, 0, 1, 1, 1, 1, 1, 1, 1)
+GM_FIRST = 1
+TT_ENG = "VSSSSSSSSSVVVVSSVV"
+AT_SLOT = (0, 0, 1, 1, 1, 1, 1, 1, 4, 4, 6, 7, 10, 10, 12, 15)
+AC_ENG = "SSSSSSSSSVSSVSSS"
+W_SLOT = (-1, -1, 0, 0, 1, 1, 3, 3)
+W_ENG = "SSSVVVVVSVVSVSVV"
 WQ_LAG = 0
-AQ_LAG = 1
-SUM_RUNS = (4, 4, 4, 4)
+AQ_LAG = 0
+PAIRS = ((0, 0), (1, 0), (2, 0), (3, 0), (0, 1), (1, 1), (2, 1))
+SUM_RUNS = (4, 4, 4, 3, 1)
 
 
 def tile_relation_trilinear_score_f4_kernel(
@@ -51,17 +53,15 @@ def tile_relation_trilinear_score_f4_kernel(
 
         scale_raw = keep.tile([128, 2, 4], F32, name="scale_raw")
         nc.scalar.dma_start(out=scale_raw[:], in_=x_scale.rearrange("o (k p t) -> p (o k) t", k=2, p=128))
+        zeros = keep.tile([128, 512], BF16, name="zeros")
+        nc.vector.memset(zeros[:], 0.0)
         gain_rows = keep.tile([128, T], BF16, name="gain_rows")
         nc.vector.memset(gain_rows[:], 0.0)
-        for role in range(2):
-            nc.scalar.dma_start(out=gain_rows[role:role + 1, :], in_=g_in[role].rearrange("(o t) -> o t", o=1))
         warm = keep.tile([128, 1], F32, name="warm")
         nc.vector.memset(warm[:], 0.0)
         nc.scalar.activation(out=warm[:], in_=warm[:], func=ACT.Tanh)
         vecs = keep.tile([128, 128], BF16, name="vecs")
         nc.vector.memset(vecs[:], 0.0)
-        for role in range(2):
-            nc.scalar.dma_start(out=vecs[8 * role:8 * role + 8, :], in_=b_in[role].rearrange("(t q) -> t q", q=128))
 
         x_view = x_bytes.rearrange("(g p j) k -> g p j k", p=128, j=4)
         x_raw = [keep.tile([128, 4, K], U8, name="x_raw%d" % g) for g in range(2)]
@@ -71,13 +71,13 @@ def tile_relation_trilinear_score_f4_kernel(
             nc.sync.dma_start(out=x_raw[g][:, 2 * u:2 * u + 2, :], in_=x_view[g, :, 2 * u:2 * u + 2, :])
 
         def load_w(role, kk, dh):
-            t = work.tile([128, 4, 512], BF16, name="raw", tag="raw", bufs=9, align_bytes=64)
+            t = work.tile([128, 4, 512], BF16, name="raw", tag="raw", bufs=10, align_bytes=64)
             view = w_in[role][kk * 512:(kk + 1) * 512, dh * 512:(dh + 1) * 512]
             nc.sync.dma_start(out=t[:], in_=view.rearrange("(p j) d -> p j d", j=4))
             w_raw[role, kk, dh] = t
 
         def load_a(role, pp):
-            t = work.tile([128, 2, T], BF16, name="raw", tag="raw", bufs=9, align_bytes=64)
+            t = work.tile([128, 2, T], BF16, name="raw", tag="raw", bufs=10, align_bytes=64)
             nc.sync.dma_start(out=t[:], in_=a_in[role][pp * 256:(pp + 1) * 256, :].rearrange("(s p) t -> p s t", p=128))
             a_raw[role, pp] = t
 
@@ -95,8 +95,12 @@ def tile_relation_trilinear_score_f4_kernel(
         ident_bf = keep.tile([128, 128], BF16, name="ident_bf")
         make_identity(nc, ident_bf[:])
 
+        for role in range(2):
+            nc.gpsimd.dma_start(out=vecs[8 * role:8 * role + 8, :], in_=b_in[role].rearrange("(t q) -> t q", q=128))
+        for role in range(2):
+            nc.gpsimd.dma_start(out=gain_rows[role:role + 1, :], in_=g_in[role].rearrange("(o t) -> o t", o=1))
         rel_bf = keep.tile([128, C], BF16, name="rel_bf")
-        nc.scalar.dma_start(out=rel_bf[:], in_=rel)
+        nc.gpsimd.dma_start(out=rel_bf[:], in_=rel)
         beta_bc = keep.tile([128, R], BF16, name="beta_bc")
         scale8 = keep.tile([128, 2, 2, 4], F32, name="scale8")
 
@@ -104,6 +108,7 @@ def tile_relation_trilinear_score_f4_kernel(
         b_t = keep.tile([128, 16], BF16, name="b_t")
 
         S = {}
+        merged = set()
 
         def codes(nm, width, **kw):
             c = keep.tile([128, width], U32, name=nm + "_codes", align_bytes=64, **kw)
@@ -170,33 +175,19 @@ def tile_relation_trilinear_score_f4_kernel(
             for kk in range(2):
                 xs(1, u, kk)
 
-        def wt(role, kk, q):
-            bank = psum.tile([128, 1024], BF16, name="tr", tag="tr", bufs=4)
-            for h in range(2):
-                d0 = 256 * (q % 2) + 128 * h
-                nc.tensor.matmul(
-                    bank[:, 512 * h:512 * (h + 1)], lhsT=ident_bf[:],
-                    rhs=w_raw[role, kk, q // 2][:, :, d0:d0 + 128].rearrange("p j d -> p d j"), start=True, stop=True,
-                )
-            S["wt", role, kk, q] = bank
-
         def xq(g, kk):
             S["xq", g, kk] = codes("xq%d%d" % (g, kk), 512)
             quantize(S["xq", g, kk], S["xg", g, kk][:].rearrange("p u n -> p (u n)"))
 
         def wi(role, kk, q, eng):
-            t = work.tile([128, 256, 4], BF16, name="wg", tag="wg", bufs=6, align_bytes=64)
-            if role == 0 and q in W_ON_TENSOR:
-                wt(role, kk, q)
-                copy(eng, t[:].rearrange("p d j -> p (d j)"), S["wt", role, kk, q][:])
-            else:
-                src = w_raw[role, kk, q // 2][:, :, 256 * (q % 2):256 * (q % 2 + 1)]
-                copy(eng, t[:], src.rearrange("p j d -> p d j"))
-            S["wi", role, kk, q] = t
+            if kk == 0:
+                S["wi", role, q] = work.tile([128, 2, 256, 4], BF16, name="wg", tag="wg", bufs=3, align_bytes=64)
+            src = w_raw[role, kk, q // 2][:, :, 256 * (q % 2):256 * (q % 2 + 1)]
+            copy(eng, S["wi", role, q][:, kk], src.rearrange("p j d -> p d j"))
 
-        def wq(role, kk, q):
-            S["wq", role, kk, q] = codes("wq%d%d" % (kk, q), 256, bufs=2)
-            quantize(S["wq", role, kk, q], S["wi", role, kk, q][:].rearrange("p d j -> p (d j)"))
+        def wq(role, q):
+            S["wq", role, q] = codes("wq%d" % q, 512, bufs=2)
+            quantize(S["wq", role, q], S["wi", role, q][:].rearrange("p k d j -> p (k d j)"))
 
         def at(role, g, pp):
             words = a_raw[role, pp][:].rearrange("p s t -> p (s t)").bitcast(F32)
@@ -220,29 +211,40 @@ def tile_relation_trilinear_score_f4_kernel(
 
         def mm(role, g, dt):
             acc = psum.tile([128, 512], F32, name="mm", tag="mm", bufs=4)
-            cols = slice(128 * (dt % 2), 128 * (dt % 2 + 1))
             for kk in range(2):
-                mx(acc[:], S["wq", role, kk, dt // 2], cols, S["xq", g, kk], kk == 0, kk == 1)
+                d0 = 256 * kk + 128 * (dt % 2)
+                mx(acc[:], S["wq", role, dt // 2], slice(d0, d0 + 128), S["xq", g, kk], kk == 0, kk == 1)
             S["mm", role, g, dt] = acc
 
         def th(role, g, dt):
-            t = work.tile([128, 512], F32, name="th", tag="th", bufs=6)
+            if dt % 2 == 0:
+                S["th", role, g, dt] = work.tile([128, 2, 512], F32, name="th", tag="th", bufs=4)
             col = 8 * role + dt
-            nc.scalar.activation(out=t[:], in_=S["mm", role, g, dt][:], func=ACT.Tanh, bias=b_t[:, col:col + 1])
-            S["th", role, g, dt] = t
+            nc.scalar.activation(
+                out=S["th", role, g, dt - dt % 2][:, dt % 2, :], in_=S["mm", role, g, dt][:], func=ACT.Tanh,
+                bias=b_t[:, col:col + 1],
+            )
 
         def gm(role, g, dt):
-            t = work.tile([128, 512], BF16, name="gm", tag="gm", bufs=6, align_bytes=64)
-            nc.vector.tensor_tensor(out=t[:], in0=S["th", role, g, dt][:], in1=S["gain", role, g][:], op=ALU.mult)
+            t = work.tile([128, 2, 512], BF16, name="gm", tag="gm", bufs=4, align_bytes=64)
+            gain = S["gain", role, g][:].unsqueeze(1).to_broadcast([128, 2, 512])
+            nc.vector.tensor_tensor(out=t[:], in0=S["th", role, g, dt][:], in1=gain, op=ALU.mult)
             S["gm", role, g, dt] = t
 
         def ht(role, g, dt):
             bank = psum.tile([128, 2, 256], F32, name="tr", tag="tr", bufs=4)
             for s in range(2):
-                words = S["gm", role, g, dt + s][:].bitcast(F32)
+                words = S["gm", role, g, dt][:, s, :].bitcast(F32)
                 for u in range(2):
                     nc.tensor.transpose(bank[:, u, 128 * s:128 * (s + 1)], words[:, 128 * u:128 * (u + 1)], ident[:])
             S["ht", role, g, dt] = bank
+
+        def dm(n):
+            if n == 0:
+                return
+            bank = psum.tile([128, 512], F32, name="mm", tag="mm", bufs=4)
+            for k in range(n):
+                nc.tensor.matmul(bank[:], lhsT=zeros[:, 0:128], rhs=zeros[:], start=True, stop=True)
 
         def tt(role, g, dt, eng):
             if dt == 0:
@@ -269,17 +271,27 @@ def tile_relation_trilinear_score_f4_kernel(
             nc.scalar.activation(out=S["es", c, ph], in_=S["pm", 0, c, ph][:], func=ACT.Copy, scale=rel_f[:, c:c + 1])
 
         def ev(c, ph):
-            t = work.tile([128, 512], F32, name="prod", tag="prod", bufs=8)
-            nc.vector.tensor_tensor(out=t[:], in0=S["pm", 1, c, ph][:], in1=S["es", c, ph], op=ALU.mult)
+            if c % 2 == 0:
+                S["prod", c // 2, ph] = work.tile([128, 2, 512], F32, name="prod", tag="raw", bufs=10, align_bytes=64)
+            t = S["prod", c // 2, ph][:, c % 2, :]
+            nc.vector.tensor_tensor(out=t, in0=S["pm", 1, c, ph][:], in1=S["es", c, ph], op=ALU.mult)
             S["ev", c, ph] = t
 
+        def pair(c, ph):
+            t = S["ev", c - 1, ph]
+            nc.gpsimd.tensor_tensor(out=t, in0=t, in1=S["ev", c, ph], op=ALU.add)
+            merged.add((c, ph))
+
         def st(c, ph):
+            if (c, ph) in merged:
+                return
+            last = C - 2 if (C - 1, ph) in merged else C - 1
             for m in range(4):
                 if c == 0:
                     S["sum", ph, m] = psum.tile([128, 128], F32, name="tr", tag="tr", bufs=4)
                 nc.tensor.matmul(
                     S["sum", ph, m][:], lhsT=S["ev", c, ph][:, 128 * m:128 * (m + 1)], rhs=ident[:],
-                    is_transpose=True, start=(c == 0), stop=(c == C - 1),
+                    is_transpose=True, start=(c == 0), stop=(c == last),
                 )
 
         def fin(ph):
@@ -298,55 +310,75 @@ def tile_relation_trilinear_score_f4_kernel(
             load_a(1, pp)
 
         ctx.enter_context(tc.manual_schedule())
+        dm(DM[0])
         wd(0, 0, "V")
         wd(0, 1, "S")
-        b_ps = psum.tile([128, 128], BF16, name="tr", tag="tr", bufs=4)
-        nc.tensor.transpose(b_ps[:], vecs[:], ident_bf[:])
         nc.vector.tensor_copy(out=scale8[:], in_=scale_raw[:].unsqueeze(2).to_broadcast([128, 2, 2, 4]))
-        for kk in range(2):
-            for u in range(2):
-                xt(0, u, kk)
-        nc.vector.tensor_copy(out=b_t[:], in_=b_ps[:, 0:16])
+        for u in range(2):
+            xt(0, u, 0)
+        dm(DM[1])
+        for u in range(2):
+            xt(0, u, 1)
+        dm(DM[2])
         wi(0, 0, 0, "S")
         wi(0, 1, 0, Q0_ENG)
-        if not GAIN_LATE:
-            gp(0, 0)
-            gb(0, 0)
         xs(0, 0, 0)
         xs(0, 1, 0)
         xq(0, 0)
-        wq(0, 0, 0)
-        wq(0, 1, 0)
+        wq(0, 0)
         if SWAP:
             wd(1, 0, "S")
         wi(0, 0, 1, "S")
-        wi(0, 1, 1, "S")
+        wi(0, 1, 1, Q1_ENG)
         xs(0, 0, 1)
         xs(0, 1, 1)
         xq(0, 1)
-        wq(0, 0, 1)
-        wq(0, 1, 1)
+        wq(0, 1)
         if not SWAP:
             wd(1, 0, "S")
         wd(1, 1, "S")
+        b_ps = psum.tile([128, 128], BF16, name="tr", tag="tr", bufs=4)
+        nc.tensor.transpose(b_ps[:], vecs[:], ident_bf[:])
+        nc.scalar.copy(out=b_t[:], in_=b_ps[:, 0:16])
+        for g in range(2):
+            gp(0, g)
+            gb(0, g)
+        dm(DM[3])
         for u in range(2):
             if X1_SLOT[u] < 0:
                 x1(u)
-        if GAIN_LATE:
-            gp(0, 0)
-            gb(0, 0)
-        gp(0, 1)
-        gb(0, 1)
+                dm(DM[4 + u])
         nc.vector.tensor_copy(out=rel_f[:], in_=rel_bf[:])
         quads = [(role, g, half) for role in range(2) for g in range(2) for half in range(2)]
         banks = [(role, g, pp) for role in range(2) for pp in range(4) for g in range(2)]
         halves = [(ph, c) for ph in range(2) for c in range(C)]
 
-        def a_run(run):
+        def a_run(slot):
+            run = [n for n in range(16) if AT_SLOT[n] == slot]
             for n in run:
                 at(*banks[n])
             for n in run:
                 ac(*banks[n], AC_ENG[n])
+
+        def h_run(i):
+            if i == 0:
+                return
+            role, g, half = quads[i - 1]
+            for dt in (4 * half, 4 * half + 2):
+                ht(role, g, dt)
+            for n, dt in enumerate((4 * half, 4 * half + 2)):
+                tt(role, g, dt, TT_ENG[2 * i + n])
+
+        def mm_run(i, d0):
+            role, g, half = quads[i]
+            for dt in (4 * half + d0, 4 * half + d0 + 1):
+                mm(role, g, dt)
+            for dt in (4 * half + d0, 4 * half + d0 + 1):
+                th(role, g, dt)
+
+        def gm_at(i, d0):
+            role, g, half = quads[i]
+            gm(role, g, 4 * half + d0)
 
         first = 0
         for i in range(9):
@@ -360,45 +392,45 @@ def tile_relation_trilinear_score_f4_kernel(
                     es(c, ph)
 
             if i < 8:
-                role, g, half = quads[i]
-                for dt in range(4 * half, 4 * half + 4):
-                    mm(role, g, dt)
-                for dt in range(4 * half, 4 * half + 4):
-                    th(role, g, dt)
+                mm_run(i, 0)
+                if HT_LATE[i] == 0:
+                    h_run(i)
+                a_run(3 * i)
+                if i < 6:
+                    dm(DM[6 + 2 * i])
+                mm_run(i, 2)
                 eh_run()
-            if i == GP_SLOT:
-                for g in range(2):
-                    gp(1, g)
-                    gb(1, g)
-            for u in range(2):
-                if X1_SLOT[u] == i:
-                    x1(u)
-            run = [n for n in range(16) if AT_SLOT[n] == i]
-            a_run(run[:AT_FIRST])
-            if i >= 1:
-                role, g, half = quads[i - 1]
-                for dt in (4 * half, 4 * half + 2):
-                    ht(role, g, dt)
-                for n, dt in enumerate((4 * half, 4 * half + 2)):
-                    tt(role, g, dt, TT_ENG[2 * i + n])
-            if i == 8:
+                if i < 6:
+                    dm(DM[7 + 2 * i])
+                if i == GP_SLOT:
+                    for g in range(2):
+                        gp(1, g)
+                        gb(1, g)
+                for u in range(2):
+                    if X1_SLOT[u] == i:
+                        x1(u)
+                        dm(DM[4 + u])
+                if GM_FIRST:
+                    gm_at(i, 0)
+                if HT_LATE[i] == 1:
+                    h_run(i)
+                a_run(3 * i + 1)
+                if i == max(0, max(X1_SLOT) + XQ_LAG):
+                    xq(1, 0)
+                    xq(1, 1)
+                if not GM_FIRST:
+                    gm_at(i, 0)
+                gm_at(i, 2)
+            else:
+                h_run(i)
                 eh_run()
-            if i == max(0, max(X1_SLOT) + XQ_LAG):
-                xq(1, 0)
-                xq(1, 1)
-            if i < 8:
-                role, g, half = quads[i]
-                for dt in range(4 * half, 4 * half + 4):
-                    gm(role, g, dt)
-            a_run(run[AT_FIRST:])
             for role in range(2):
                 for q in range(4):
                     if W_SLOT[4 * role + q] == i:
                         for kk in range(2):
                             wi(role, kk, q, W_ENG[8 * role + 2 * q + kk])
                     if W_SLOT[4 * role + q] >= 0 and W_SLOT[4 * role + q] + WQ_LAG == i:
-                        for kk in range(2):
-                            wq(role, kk, q)
+                        wq(role, q)
             if i >= 1 and quads[i - 1][2] == 1:
                 role, g, half = quads[i - 1]
                 for ch in range(2):
@@ -406,7 +438,7 @@ def tile_relation_trilinear_score_f4_kernel(
             for role in range(2):
                 for ph in range(2):
                     for g in range(2):
-                        last = max(AT_SLOT[8 * role + 2 * pp + g] for pp in (2 * ph, 2 * ph + 1))
+                        last = max(AT_SLOT[8 * role + 2 * pp + g] for pp in (2 * ph, 2 * ph + 1)) // 3
                         if last + AQ_LAG == i:
                             aq(role, g, ph)
         done = 0
@@ -418,6 +450,8 @@ def tile_relation_trilinear_score_f4_kernel(
                 pm(1, c, ph)
             for ph, c in now:
                 ev(c, ph)
+                if c % 2 == 1 and (c // 2, ph) in PAIRS:
+                    pair(c, ph)
             for ph, c in before:
                 st(c, ph)
                 if c == C - 1:

@@ -3,7 +3,7 @@ from contextlib import ExitStack
 import concourse.mybir as mybir
 from concourse.masks import make_identity
 
-T, K, D, P, R = 1024, 1024, 1024, 1024, 128
+T, K, D, R = 1024, 1024, 1024, 128
 C = D // R
 FLOPS = 4 * 2 * 1024 * 1024 * 1024
 
@@ -16,444 +16,468 @@ FP8X4 = mybir.dt.float8_e4m3fn_x4
 ACT = mybir.ActivationFunctionType
 ALU = mybir.AluOpType
 
-X1_SLOT = (-1, -1)
-XQ_LAG = 0
-Q0_ENG = "S"
-Q1_ENG = "V"
-SWAP = 1
-GP_SLOT = 0
-DM = (5, 1, 0, 4, 3, 0, 0, 0, 0, 0, 0, 0, 0, 0, 0, 0, 0, 0)
-EH_COUNT = (0, 0, 0, 0, 0, 0, 4, 8, 4)
-HT_LATE = (1, 0, 1, 1, 1, 1, 1, 1, 1)
-GM_FIRST = 1
-TT_ENG = "VSSSSSSSSSVVVVSSVV"
-AT_SLOT = (0, 0, 1, 1, 1, 1, 1, 1, 4, 4, 6, 7, 10, 10, 12, 15)
-AC_ENG = "SSSSSSSSSVSSVSSS"
-W_SLOT = (-1, -1, 0, 0, 1, 1, 3, 3)
-W_ENG = "SSSVVVVVSVVSVSVV"
-WQ_LAG = 0
-AQ_LAG = 0
-PAIRS = ((0, 0), (1, 0), (2, 0), (3, 0), (0, 1), (1, 1), (2, 1))
-SUM_RUNS = (4, 4, 4, 3, 1)
+HEAD, TAIL = 0, 1
+
+SLOTS = (
+    (HEAD, 0, 0), (HEAD, 1, 0), (TAIL, 0, 0), (TAIL, 1, 0), (HEAD, 0, 1), (HEAD, 1, 1), (TAIL, 0, 1), (TAIL, 1, 1),
+)
+H_EARLY = (1, 5, 7)
+A_BETWEEN = (2, 0, 2, 0, 0, 0, 2, 0)
+A_BEHIND = (2, 4, 2, 1, 1, 0, 0, 0)
+W_PREP = (
+    ((TAIL, 0), (TAIL, 1)), ((HEAD, 3),), ((HEAD, 2),), ((TAIL, 2),), ((TAIL, 3),), (), (), (),
+)
+EH_TILES = (0, 0, 0, 0, 5, 3, 0, 5, 0, 2, 1, 0)
+ET_TILES = (0, 0, 0, 0, 0, 2, 0, 0, 0, 7, 7, 0)
+LOADS = (
+    ("w", TAIL, 0, 0), ("w", TAIL, 1, 0), ("a", HEAD, 0), ("a", HEAD, 1), ("a", HEAD, 2), ("a", HEAD, 3),
+    ("w", HEAD, 0, 1), ("w", HEAD, 1, 1), ("a", TAIL, 0), ("a", TAIL, 1), ("a", TAIL, 2), ("a", TAIL, 3),
+    ("w", TAIL, 0, 1), ("w", TAIL, 1, 1),
+)
+
+W_ON_SCALAR = ((HEAD, 0, 0), (HEAD, 1, 0), (HEAD, 0, 1), (HEAD, 1, 2), (TAIL, 0, 1))
+H_ON_VECTOR = ((1, 0), (4, 0), (4, 2), (6, 0), (7, 0))
+A_ON_VECTOR = ((HEAD, 1, 3),)
 
 
 def tile_relation_trilinear_score_f4_kernel(
     tc, x_bytes, x_scale, w_head, b_head, g_head, a_head, w_tail, b_tail, g_tail, a_tail, rel, beta, out
 ):
     nc = tc.nc
-    w_in = (w_head, w_tail)
-    a_in = (a_head, a_tail)
-    g_in = (g_head, g_tail)
-    b_in = (b_head, b_tail)
+    w_in, b_in, g_in, a_in = (w_head, w_tail), (b_head, b_tail), (g_head, g_tail), (a_head, a_tail)
 
     with ExitStack() as ctx:
         keep = ctx.enter_context(tc.tile_pool(name="keep", bufs=1))
         work = ctx.enter_context(tc.tile_pool(name="work", bufs=2))
         psum = ctx.enter_context(tc.psum_pool(name="psum", bufs=4))
 
-        scale_raw = keep.tile([128, 2, 4], F32, name="scale_raw")
-        nc.scalar.dma_start(out=scale_raw[:], in_=x_scale.rearrange("o (k p t) -> p (o k) t", k=2, p=128))
+        def raw_tile(shape, dtype, nm):
+            return work.tile(shape, dtype, name=nm, tag="raw", bufs=10, align_bytes=64)
+
+        def big_tile(shape, dtype, nm):
+            return work.tile(shape, dtype, name=nm, tag="big", bufs=8, align_bytes=64)
+
+        def product_bank():
+            return psum.tile([128, 512], F32, name="product", tag="product", bufs=4)
+
+        def turn_bank(shape, dtype=F32):
+            return psum.tile(shape, dtype, name="turn", tag="turn", bufs=4)
+
+        scale_in = keep.tile([128, 2, 4], F32, name="scale_in")
+        nc.scalar.dma_start(out=scale_in[:], in_=x_scale.rearrange("o (k p t) -> p (o k) t", k=2, p=128))
         zeros = keep.tile([128, 512], BF16, name="zeros")
         nc.vector.memset(zeros[:], 0.0)
         gain_rows = keep.tile([128, T], BF16, name="gain_rows")
         nc.vector.memset(gain_rows[:], 0.0)
-        warm = keep.tile([128, 1], F32, name="warm")
-        nc.vector.memset(warm[:], 0.0)
-        nc.scalar.activation(out=warm[:], in_=warm[:], func=ACT.Tanh)
-        vecs = keep.tile([128, 128], BF16, name="vecs")
-        nc.vector.memset(vecs[:], 0.0)
+        first_tanh = keep.tile([128, 1], F32, name="first_tanh")
+        nc.vector.memset(first_tanh[:], 0.0)
+        nc.scalar.activation(out=first_tanh[:], in_=first_tanh[:], func=ACT.Tanh)
+        bias_rows = keep.tile([128, 128], BF16, name="bias_rows")
+        nc.vector.memset(bias_rows[:], 0.0)
 
+        x_in = [keep.tile([128, 4, K], U8, name="x_in%d" % g) for g in range(2)]
         x_view = x_bytes.rearrange("(g p j) k -> g p j k", p=128, j=4)
-        x_raw = [keep.tile([128, 4, K], U8, name="x_raw%d" % g) for g in range(2)]
         w_raw, a_raw = {}, {}
 
         def load_x(g, u):
-            nc.sync.dma_start(out=x_raw[g][:, 2 * u:2 * u + 2, :], in_=x_view[g, :, 2 * u:2 * u + 2, :])
+            nc.sync.dma_start(out=x_in[g][:, 2 * u:2 * u + 2, :], in_=x_view[g, :, 2 * u:2 * u + 2, :])
 
         def load_w(role, kk, dh):
-            t = work.tile([128, 4, 512], BF16, name="raw", tag="raw", bufs=10, align_bytes=64)
-            view = w_in[role][kk * 512:(kk + 1) * 512, dh * 512:(dh + 1) * 512]
+            t = raw_tile([128, 4, 512], BF16, "w_raw")
+            view = w_in[role][512 * kk:512 * (kk + 1), 512 * dh:512 * (dh + 1)]
             nc.sync.dma_start(out=t[:], in_=view.rearrange("(p j) d -> p j d", j=4))
             w_raw[role, kk, dh] = t
 
-        def load_a(role, pp):
-            t = work.tile([128, 2, T], BF16, name="raw", tag="raw", bufs=10, align_bytes=64)
-            nc.sync.dma_start(out=t[:], in_=a_in[role][pp * 256:(pp + 1) * 256, :].rearrange("(s p) t -> p s t", p=128))
-            a_raw[role, pp] = t
+        def load_a(role, rows):
+            t = raw_tile([128, 2, T], BF16, "a_raw")
+            view = a_in[role][256 * rows:256 * (rows + 1), :]
+            nc.sync.dma_start(out=t[:], in_=view.rearrange("(s p) t -> p s t", p=128))
+            a_raw[role, rows] = t
 
         load_x(0, 0)
         load_x(0, 1)
-        load_w(0, 0, 0)
-        load_w(0, 1, 0)
+        load_w(HEAD, 0, 0)
+        load_w(HEAD, 1, 0)
+        for role in (HEAD, TAIL):
+            nc.sync.dma_start(out=gain_rows[role:role + 1, :], in_=g_in[role].rearrange("(o t) -> o t", o=1))
+        for role in (HEAD, TAIL):
+            nc.sync.dma_start(out=bias_rows[8 * role:8 * role + 8, :], in_=b_in[role].rearrange("(t q) -> t q", q=128))
         load_x(1, 0)
         load_x(1, 1)
-        load_w(0, 0, 1)
-        load_w(0, 1, 1)
+        rel_in = keep.tile([128, C], BF16, name="rel_in")
+        nc.sync.dma_start(out=rel_in[:], in_=rel)
 
         ident = keep.tile([128, 128], F32, name="ident")
         make_identity(nc, ident[:])
         ident_bf = keep.tile([128, 128], BF16, name="ident_bf")
         make_identity(nc, ident_bf[:])
+        pick = keep.tile([128, 2, 128], BF16, name="pick")
+        for hd in range(2):
+            nc.gpsimd.tensor_copy(
+                out=pick[:, hd, :].rearrange("p (c r) -> p c r", c=2),
+                in_=ident_bf[:, 64 * hd:64 * (hd + 1)].unsqueeze(1).to_broadcast([128, 2, 64]),
+            )
+        beta_row = keep.tile([128, 2, 128], BF16, name="beta_row")
+        nc.gpsimd.memset(beta_row[:], 0.0)
 
-        for role in range(2):
-            nc.gpsimd.dma_start(out=vecs[8 * role:8 * role + 8, :], in_=b_in[role].rearrange("(t q) -> t q", q=128))
-        for role in range(2):
-            nc.gpsimd.dma_start(out=gain_rows[role:role + 1, :], in_=g_in[role].rearrange("(o t) -> o t", o=1))
-        rel_bf = keep.tile([128, C], BF16, name="rel_bf")
-        nc.gpsimd.dma_start(out=rel_bf[:], in_=rel)
-        beta_bc = keep.tile([128, R], BF16, name="beta_bc")
-        scale8 = keep.tile([128, 2, 2, 4], F32, name="scale8")
+        scale_x = keep.tile([128, 2, 2, 4], F32, name="scale_x")
+        bias = keep.tile([128, 16], BF16, name="bias")
+        rel_col = keep.tile([128, 8], F32, name="rel_col")
 
-        rel_f = keep.tile([128, C], F32, name="rel_f")
-        b_t = keep.tile([128, 16], BF16, name="b_t")
+        for load in LOADS:
+            if load[0] == "w":
+                load_w(*load[1:])
+            else:
+                load_a(*load[1:])
+        nc.sync.dma_start(out=beta_row[0:1, :, 0:64], in_=beta.rearrange("(o h r) -> o h r", o=1, h=2))
 
-        S = {}
-        merged = set()
+        made = {}
 
-        def codes(nm, width, **kw):
-            c = keep.tile([128, width], U32, name=nm + "_codes", align_bytes=64, **kw)
-            s = keep.tile([128, width], U8, name=nm + "_scales", align_bytes=64, **kw)
+        def codes(nm, bufs=1):
+            c = keep.tile([128, 512], U32, name=nm + "_codes", align_bytes=64, bufs=bufs)
+            s = keep.tile([128, 512], U8, name=nm + "_scales", align_bytes=64, bufs=bufs)
             return c, s
 
         def quantize(dst, src):
             nc.vector.quantize_mx(out=dst[0][:].bitcast(FP8X4), scales=dst[1][:], in_=src)
 
-        def mx(acc, lhs, lcols, rhs, start, stop):
+        def mx_pass(acc, lhs, col, rhs, g):
+            cols = slice(col, col + 128)
             nc.tensor.matmul_mx(
-                out=acc, lhsT=lhs[0][:, lcols].bitcast(FP8X4), lhsT_scale=lhs[1][:, lcols],
-                rhs=rhs[0][:].bitcast(FP8X4), rhs_scale=rhs[1][:], start=start, stop=stop,
+                out=acc[:], lhsT=lhs[0][:, cols].bitcast(FP8X4), lhsT_scale=lhs[1][:, cols],
+                rhs=rhs[0][:].bitcast(FP8X4), rhs_scale=rhs[1][:], start=(g == 0), stop=(g == 1),
             )
 
-        def copy(eng, out_ap, in_ap):
-            if eng == "S":
-                nc.scalar.copy(out=out_ap, in_=in_ap)
+        def copy(on_vector, dst, src):
+            if on_vector:
+                nc.vector.tensor_copy(out=dst, in_=src)
             else:
-                nc.vector.tensor_copy(out=out_ap, in_=in_ap)
+                nc.scalar.copy(out=dst, in_=src)
 
-        def wd(g, u, eng):
-            t = work.tile([128, 2, K], BF16, name="xw", tag="big", bufs=8, align_bytes=64)
-            copy(eng, t[:].rearrange("p e k -> p (e k)"), x_raw[g][:, 2 * u:2 * u + 2, :].rearrange("p e k -> p (e k)").bitcast(FP8))
-            S["wd", g, u] = t
+        def row_to_all(row):
+            return ident_bf[:, row:row + 1].to_broadcast([128, 128])
 
-        def xt(g, u, kk):
-            bank = psum.tile([128, 2, 2, 128], F32, name="tr", tag="tr", bufs=4)
+        def warm(n):
+            bank = product_bank()
+            for k in range(n):
+                nc.tensor.matmul(bank[:], lhsT=zeros[:, 0:128], rhs=zeros[:], start=True, stop=True)
+
+        def x_widen(g, u, on_vector):
+            t = big_tile([128, 2, K], BF16, "x_wide")
+            src = x_in[g][:, 2 * u:2 * u + 2, :].rearrange("p e k -> p (e k)").bitcast(FP8)
+            copy(on_vector, t[:].rearrange("p e k -> p (e k)"), src)
+            made["x_wide", g, u] = t
+
+        def x_turn(g, u, kk):
+            bank = turn_bank([128, 2, 2, 128])
             for e in range(2):
-                words = S["wd", g, u][:, e, :].bitcast(F32)
+                words = made["x_wide", g, u][:, e, :].bitcast(F32)
                 for v in range(2):
                     nc.tensor.transpose(bank[:, e, v, :], words[:, 256 * kk + v:256 * (kk + 1):2], ident[:])
-            S["xt", g, u, kk] = bank
+            made["x_turn", g, u, kk] = bank
 
-        def xs(g, u, kk):
+        def x_scaled(g, u, kk):
             if u == 0:
-                S["xg", g, kk] = work.tile([128, 2, 1024], BF16, name="xg", tag="big", bufs=8, align_bytes=64)
+                made["x_rows", g, kk] = big_tile([128, 2, 1024], BF16, "x_rows")
+            bank = made["x_turn", g, u, kk][:].rearrange("p e v q -> p (e v q)").bitcast(BF16)
+            scales = scale_x[:, kk].rearrange("p e t -> p (e t)").rearrange("p (w b) -> p w b", b=2)
             nc.vector.tensor_tensor(
-                out=S["xg", g, kk][:, u, :].rearrange("p (q w b) -> p q w b", w=4, b=2),
-                in0=S["xt", g, u, kk][:].rearrange("p e v q -> p (e v q)").bitcast(BF16).rearrange("p (w q b) -> p q w b", w=4, b=2),
-                in1=scale8[:, kk].rearrange("p e t -> p (e t)").rearrange("p (w b) -> p w b", b=2).unsqueeze(1).to_broadcast([128, 128, 4, 2]),
+                out=made["x_rows", g, kk][:, u, :].rearrange("p (q w b) -> p q w b", w=4, b=2),
+                in0=bank.rearrange("p (w q b) -> p q w b", w=4, b=2),
+                in1=scales.unsqueeze(1).to_broadcast([128, 128, 4, 2]),
                 op=ALU.mult,
             )
 
-        def gp(role, g):
-            bank = psum.tile([128, 512], F32, name="tr", tag="tr", bufs=4)
-            nc.tensor.matmul(
-                bank[:], lhsT=ident_bf[:, role:role + 1].to_broadcast([128, 128]),
-                rhs=gain_rows[:, 512 * g:512 * (g + 1)], start=True, stop=True,
-            )
-            S["gp", role, g] = bank
+        def x_quant(g, kk):
+            made["x", g, kk] = codes("x%d%d" % (g, kk))
+            quantize(made["x", g, kk], made["x_rows", g, kk][:].rearrange("p u n -> p (u n)"))
 
-        def gb(role, g):
+        def gain_spread(role, g):
+            bank = turn_bank([128, 512])
+            nc.tensor.matmul(
+                bank[:], lhsT=row_to_all(role), rhs=gain_rows[:, 512 * g:512 * (g + 1)], start=True, stop=True,
+            )
             t = keep.tile([128, 512], BF16, name="gain%d%d" % (role, g), align_bytes=64)
             nc.scalar.copy(
                 out=t[:].rearrange("p (u q e) -> p u q e", u=2, e=2),
-                in_=S["gp", role, g][:].rearrange("p (q u e) -> p u q e", u=2, e=2),
+                in_=bank[:].rearrange("p (q u e) -> p u q e", u=2, e=2),
             )
-            S["gain", role, g] = t
+            made["gain", role, g] = t
 
-        def x1(u):
-            for kk in range(2):
-                xt(1, u, kk)
-            for kk in range(2):
-                xs(1, u, kk)
-
-        def xq(g, kk):
-            S["xq", g, kk] = codes("xq%d%d" % (g, kk), 512)
-            quantize(S["xq", g, kk], S["xg", g, kk][:].rearrange("p u n -> p (u n)"))
-
-        def wi(role, kk, q, eng):
+        def w_rows(role, kk, quarter):
             if kk == 0:
-                S["wi", role, q] = work.tile([128, 2, 256, 4], BF16, name="wg", tag="wg", bufs=3, align_bytes=64)
-            src = w_raw[role, kk, q // 2][:, :, 256 * (q % 2):256 * (q % 2 + 1)]
-            copy(eng, S["wi", role, q][:, kk], src.rearrange("p j d -> p d j"))
+                made["w_rows", role, quarter] = work.tile(
+                    [128, 2, 256, 4], BF16, name="w_rows", tag="w_rows", bufs=3, align_bytes=64,
+                )
+            d0 = 256 * (quarter % 2)
+            src = w_raw[role, kk, quarter // 2][:, :, d0:d0 + 256].rearrange("p j d -> p d j")
+            copy((role, kk, quarter) not in W_ON_SCALAR, made["w_rows", role, quarter][:, kk], src)
 
-        def wq(role, q):
-            S["wq", role, q] = codes("wq%d" % q, 512, bufs=2)
-            quantize(S["wq", role, q], S["wi", role, q][:].rearrange("p k d j -> p (k d j)"))
+        def w_quant(role, quarter):
+            made["w", role, quarter] = codes("w%d" % quarter, bufs=2)
+            quantize(made["w", role, quarter], made["w_rows", role, quarter][:].rearrange("p k d j -> p (k d j)"))
 
-        def at(role, g, pp):
-            words = a_raw[role, pp][:].rearrange("p s t -> p (s t)").bitcast(F32)
-            bank = psum.tile([128, 2, 2, 128], F32, name="tr", tag="tr", bufs=4)
+        def a_turn(role, g, rows):
+            words = a_raw[role, rows][:].rearrange("p s t -> p (s t)").bitcast(F32)
+            bank = turn_bank([128, 2, 2, 128])
             for s in range(2):
                 for u in range(2):
                     w0 = 512 * s + 256 * g
                     nc.tensor.transpose(bank[:, s, u, :], words[:, w0 + u:w0 + 256:2], ident[:])
-            S["at", role, g, pp] = bank
+            made["a_turn", role, g, rows] = bank
 
-        def ac(role, g, pp, eng):
-            if pp % 2 == 0:
-                S["ag", role, g, pp // 2] = work.tile([128, 512, 4], BF16, name="ag", tag="ag", bufs=4, align_bytes=64)
-            dst = S["ag", role, g, pp // 2][:].rearrange("p n t -> p (n t)").bitcast(F32)
-            dst = dst.rearrange("p (s r u) -> p s r u", s=4, u=2)[:, 2 * (pp % 2):2 * (pp % 2) + 2]
-            copy(eng, dst, S["at", role, g, pp][:].rearrange("p s u r -> p s r u"))
+        def a_rows(role, g, rows):
+            if rows % 2 == 0:
+                made["a_rows", role, g, rows // 2] = work.tile(
+                    [128, 512, 4], BF16, name="a_rows", tag="a_rows", bufs=4, align_bytes=64,
+                )
+            dst = made["a_rows", role, g, rows // 2][:].rearrange("p n t -> p (n t)").bitcast(F32)
+            dst = dst.rearrange("p (s r u) -> p s r u", s=4, u=2)[:, 2 * (rows % 2):2 * (rows % 2) + 2]
+            src = made["a_turn", role, g, rows][:].rearrange("p s u r -> p s r u")
+            copy((role, g, rows) in A_ON_VECTOR, dst, src)
 
-        def aq(role, g, ph):
-            S["aq", role, g, ph] = codes("aq%d%d%d" % (role, g, ph), 512)
-            quantize(S["aq", role, g, ph], S["ag", role, g, ph][:].rearrange("p n t -> p (n t)"))
+        def a_quant(role, g, ph):
+            made["a", role, g, ph] = codes("a%d%d%d" % (role, g, ph))
+            quantize(made["a", role, g, ph], made["a_rows", role, g, ph][:].rearrange("p n t -> p (n t)"))
 
-        def mm(role, g, dt):
-            acc = psum.tile([128, 512], F32, name="mm", tag="mm", bufs=4)
+        def unit_matmul(role, g, dt):
+            acc = product_bank()
             for kk in range(2):
-                d0 = 256 * kk + 128 * (dt % 2)
-                mx(acc[:], S["wq", role, dt // 2], slice(d0, d0 + 128), S["xq", g, kk], kk == 0, kk == 1)
-            S["mm", role, g, dt] = acc
+                mx_pass(acc, made["w", role, dt // 2], 256 * kk + 128 * (dt % 2), made["x", g, kk], kk)
+            made["unit", role, g, dt] = acc
 
-        def th(role, g, dt):
-            if dt % 2 == 0:
-                S["th", role, g, dt] = work.tile([128, 2, 512], F32, name="th", tag="th", bufs=4)
+        def unit_tanh(role, g, dt):
+            first = dt - dt % 2
+            if dt == first:
+                made["tanh", role, g, first] = work.tile([128, 2, 512], F32, name="tanh", tag="tanh", bufs=4)
             col = 8 * role + dt
             nc.scalar.activation(
-                out=S["th", role, g, dt - dt % 2][:, dt % 2, :], in_=S["mm", role, g, dt][:], func=ACT.Tanh,
-                bias=b_t[:, col:col + 1],
+                out=made["tanh", role, g, first][:, dt - first, :], in_=made["unit", role, g, dt][:], func=ACT.Tanh,
+                bias=bias[:, col:col + 1],
             )
 
-        def gm(role, g, dt):
-            t = work.tile([128, 2, 512], BF16, name="gm", tag="gm", bufs=4, align_bytes=64)
-            gain = S["gain", role, g][:].unsqueeze(1).to_broadcast([128, 2, 512])
-            nc.vector.tensor_tensor(out=t[:], in0=S["th", role, g, dt][:], in1=gain, op=ALU.mult)
-            S["gm", role, g, dt] = t
+        def pair_gain(role, g, dt):
+            t = work.tile([128, 2, 512], BF16, name="h_cols", tag="h_cols", bufs=4, align_bytes=64)
+            gain = made["gain", role, g][:].unsqueeze(1).to_broadcast([128, 2, 512])
+            nc.vector.tensor_tensor(out=t[:], in0=made["tanh", role, g, dt][:], in1=gain, op=ALU.mult)
+            made["h_cols", role, g, dt] = t
 
-        def ht(role, g, dt):
-            bank = psum.tile([128, 2, 256], F32, name="tr", tag="tr", bufs=4)
+        def pair_turn(role, g, dt):
+            bank = turn_bank([128, 2, 256])
             for s in range(2):
-                words = S["gm", role, g, dt][:, s, :].bitcast(F32)
+                words = made["h_cols", role, g, dt][:, s, :].bitcast(F32)
                 for u in range(2):
                     nc.tensor.transpose(bank[:, u, 128 * s:128 * (s + 1)], words[:, 128 * u:128 * (u + 1)], ident[:])
-            S["ht", role, g, dt] = bank
+            made["h_turn", role, g, dt] = bank
 
-        def dm(n):
-            if n == 0:
-                return
-            bank = psum.tile([128, 512], F32, name="mm", tag="mm", bufs=4)
-            for k in range(n):
-                nc.tensor.matmul(bank[:], lhsT=zeros[:, 0:128], rhs=zeros[:], start=True, stop=True)
-
-        def tt(role, g, dt, eng):
-            if dt == 0:
-                S["hg", role, g] = work.tile([128, C, 128, 4], BF16, name="hg", tag="hg", bufs=2, align_bytes=64)
-            dst = S["hg", role, g][:].rearrange("p c r t -> p (c r t)").bitcast(F32)
-            dst = dst.rearrange("p (c r u) -> p c r u", c=C, u=2)[:, :, 16 * dt:16 * dt + 32, :]
-            copy(eng, dst, S["ht", role, g, dt][:].rearrange("p u (r c) -> p c r u", c=C))
-
-        def hq(role, g, ch):
-            S["hq", role, g, ch] = codes("hq%d%d%d" % (role, g, ch), 512)
-            quantize(S["hq", role, g, ch], S["hg", role, g][:, 4 * ch:4 * ch + 4].rearrange("p c r t -> p (c r t)"))
-
-        def pm(role, c, ph):
-            acc = psum.tile([128, 512], F32, name="mm", tag="mm", bufs=4)
-            cols = slice(128 * (c % 4), 128 * (c % 4 + 1))
-            for g in range(2):
-                mx(acc[:], S["hq", role, g, c // 4], cols, S["aq", role, g, ph], g == 0, g == 1)
-            S["pm", role, c, ph] = acc
-
-        def es(c, ph):
-            if ph == 0:
-                S["ehs", c] = work.tile([128, 2, 512], F32, name="ehs", tag="big", bufs=8, align_bytes=64)
-            S["es", c, ph] = S["ehs", c][:, ph, :]
-            nc.scalar.activation(out=S["es", c, ph], in_=S["pm", 0, c, ph][:], func=ACT.Copy, scale=rel_f[:, c:c + 1])
-
-        def ev(c, ph):
-            if c % 2 == 0:
-                S["prod", c // 2, ph] = work.tile([128, 2, 512], F32, name="prod", tag="raw", bufs=10, align_bytes=64)
-            t = S["prod", c // 2, ph][:, c % 2, :]
-            nc.vector.tensor_tensor(out=t, in0=S["pm", 1, c, ph][:], in1=S["es", c, ph], op=ALU.mult)
-            S["ev", c, ph] = t
-
-        def pair(c, ph):
-            t = S["ev", c - 1, ph]
-            nc.gpsimd.tensor_tensor(out=t, in0=t, in1=S["ev", c, ph], op=ALU.add)
-            merged.add((c, ph))
-
-        def st(c, ph):
-            if (c, ph) in merged:
-                return
-            last = C - 2 if (C - 1, ph) in merged else C - 1
-            for m in range(4):
-                if c == 0:
-                    S["sum", ph, m] = psum.tile([128, 128], F32, name="tr", tag="tr", bufs=4)
-                nc.tensor.matmul(
-                    S["sum", ph, m][:], lhsT=S["ev", c, ph][:, 128 * m:128 * (m + 1)], rhs=ident[:],
-                    is_transpose=True, start=(c == 0), stop=(c == last),
+        def pair_rows(role, g, dt, on_vector):
+            hd = dt // 4
+            if dt % 4 == 0:
+                made["h_rows", role, g, hd] = work.tile(
+                    [128, C, 64, 4], BF16, name="h_rows", tag="h_rows", bufs=4, align_bytes=64,
                 )
+            dst = made["h_rows", role, g, hd][:].rearrange("p c r t -> p (c r t)").bitcast(F32)
+            r0 = 16 * (dt % 4)
+            dst = dst.rearrange("p (c r u) -> p c r u", c=C, u=2)[:, :, r0:r0 + 32, :]
+            copy(on_vector, dst, made["h_turn", role, g, dt][:].rearrange("p u (r c) -> p c r u", c=C))
 
-        def fin(ph):
-            o = work.tile([128, 4, R], F32, name="o", tag="o", bufs=1)
+        def h_quant(role, g, hd):
+            made["h", role, g, hd] = codes("h%d%d%d" % (role, g, hd))
+            quantize(made["h", role, g, hd], made["h_rows", role, g, hd][:].rearrange("p c r t -> p (c r t)"))
+
+        def pooled(role, hd, k, ph):
+            acc = product_bank()
+            for g in range(2):
+                mx_pass(acc, made["h", role, g, hd], 128 * k, made["a", role, g, ph], g)
+            made["pooled", role, hd, k, ph] = acc
+
+        def eh_rel(hd, k, ph):
+            if ph == 0:
+                made["eh", hd, k] = big_tile([128, 2, 512], F32, "eh")
+            col = 4 * hd + k
+            nc.scalar.activation(
+                out=made["eh", hd, k][:, ph, :], in_=made["pooled", HEAD, hd, k, ph][:], func=ACT.Copy,
+                scale=rel_col[:, col:col + 1],
+            )
+
+        def added_early(hd, k, ph):
+            return (hd, k, ph) != (1, 2, 1)
+
+        def product(hd, k, ph):
+            first = k - k % 2
+            if k == first:
+                made["product", hd, first, ph] = raw_tile([128, 2, 512], F32, "product")
+            t = made["product", hd, first, ph]
+            nc.vector.tensor_tensor(
+                out=t[:, k - first, :], in0=made["pooled", TAIL, hd, k, ph][:], in1=made["eh", hd, first + k % 2][:, ph, :],
+                op=ALU.mult,
+            )
+            if k > first and added_early(hd, first, ph):
+                nc.gpsimd.tensor_tensor(out=t[:, 0, :], in0=t[:, 0, :], in1=t[:, 1, :], op=ALU.add)
+
+        def sum_turn(hd, ph):
+            terms = []
+            for k in (0, 2):
+                t = made["product", hd, k, ph]
+                terms.append(t[:, 0, :])
+                if not added_early(hd, k, ph):
+                    terms.append(t[:, 1, :])
+            bank = turn_bank([128, 4, 128])
+            nc.tensor.matmul(
+                bank[:], lhsT=row_to_all(0), rhs=beta_row[:, hd, :].unsqueeze(1).to_broadcast([128, 4, 128]),
+                start=True, stop=False,
+            )
             for m in range(4):
-                nc.vector.tensor_tensor(out=o[:, m, :], in0=S["sum", ph, m][:], in1=beta_bc[:], op=ALU.add)
-            nc.sync.dma_start(out=out[512 * ph:512 * (ph + 1), :].rearrange("(m p) r -> p m r", p=128), in_=o[:])
+                for n in range(len(terms)):
+                    nc.tensor.matmul(
+                        bank[:, m, :], lhsT=terms[n][:, 128 * m:128 * (m + 1)], rhs=ident[:],
+                        is_transpose=True, start=False, stop=(m == 3 and n == len(terms) - 1),
+                    )
+            made["sum", hd, ph] = bank
 
-        for pp in range(4):
-            load_a(0, pp)
-        nc.sync.dma_start(out=beta_bc[:], in_=beta.partition_broadcast(128))
-        for dh in range(2):
-            for kk in range(2):
-                load_w(1, kk, dh)
-        for pp in range(4):
-            load_a(1, pp)
+        def finish(hd, ph):
+            t = work.tile([128, 4, 64], F32, name="score", tag="score", bufs=2)
+            nc.vector.tensor_reduce(
+                out=t[:], in_=made["sum", hd, ph][:].rearrange("p m (c r) -> p m r c", c=2),
+                axis=mybir.AxisListType.X, op=ALU.add,
+            )
+            dst = out[512 * ph:512 * (ph + 1), 64 * hd:64 * (hd + 1)]
+            nc.sync.dma_start(out=dst.rearrange("(m p) r -> p m r", p=128), in_=t[:])
 
         ctx.enter_context(tc.manual_schedule())
-        dm(DM[0])
-        wd(0, 0, "V")
-        wd(0, 1, "S")
-        nc.vector.tensor_copy(out=scale8[:], in_=scale_raw[:].unsqueeze(2).to_broadcast([128, 2, 2, 4]))
-        for u in range(2):
-            xt(0, u, 0)
-        dm(DM[1])
-        for u in range(2):
-            xt(0, u, 1)
-        dm(DM[2])
-        wi(0, 0, 0, "S")
-        wi(0, 1, 0, Q0_ENG)
-        xs(0, 0, 0)
-        xs(0, 1, 0)
-        xq(0, 0)
-        wq(0, 0)
-        if SWAP:
-            wd(1, 0, "S")
-        wi(0, 0, 1, "S")
-        wi(0, 1, 1, Q1_ENG)
-        xs(0, 0, 1)
-        xs(0, 1, 1)
-        xq(0, 1)
-        wq(0, 1)
-        if not SWAP:
-            wd(1, 0, "S")
-        wd(1, 1, "S")
-        b_ps = psum.tile([128, 128], BF16, name="tr", tag="tr", bufs=4)
-        nc.tensor.transpose(b_ps[:], vecs[:], ident_bf[:])
-        nc.scalar.copy(out=b_t[:], in_=b_ps[:, 0:16])
+
+        warm(6)
+        x_widen(0, 0, True)
+        x_widen(0, 1, False)
+        nc.vector.tensor_copy(out=scale_x[:], in_=scale_in[:].unsqueeze(2).to_broadcast([128, 2, 2, 4]))
+        for kk in range(2):
+            for u in range(2):
+                x_turn(0, u, kk)
+        for kk in range(2):
+            w_rows(HEAD, kk, 0)
+        for kk in range(2):
+            if kk == 1:
+                x_widen(1, 0, False)
+                w_rows(HEAD, 0, 1)
+                w_rows(HEAD, 1, 1)
+            for u in range(2):
+                x_scaled(0, u, kk)
+            x_quant(0, kk)
+            w_quant(HEAD, kk)
+        x_widen(1, 1, False)
+        bias_bank = turn_bank([128, 128], BF16)
+        nc.tensor.transpose(bias_bank[:], bias_rows[:], ident_bf[:])
+        nc.scalar.copy(out=bias[:], in_=bias_bank[:, 0:16])
         for g in range(2):
-            gp(0, g)
-            gb(0, g)
-        dm(DM[3])
+            gain_spread(HEAD, g)
+        warm(1)
         for u in range(2):
-            if X1_SLOT[u] < 0:
-                x1(u)
-                dm(DM[4 + u])
-        nc.vector.tensor_copy(out=rel_f[:], in_=rel_bf[:])
-        quads = [(role, g, half) for role in range(2) for g in range(2) for half in range(2)]
-        banks = [(role, g, pp) for role in range(2) for pp in range(4) for g in range(2)]
-        halves = [(ph, c) for ph in range(2) for c in range(C)]
+            for kk in range(2):
+                x_turn(1, u, kk)
+            for kk in range(2):
+                x_scaled(1, u, kk)
+            if u == 0:
+                warm(2)
 
-        def a_run(slot):
-            run = [n for n in range(16) if AT_SLOT[n] == slot]
-            for n in run:
-                at(*banks[n])
-            for n in run:
-                ac(*banks[n], AC_ENG[n])
+        def rel_columns():
+            bank = turn_bank([128, 2, 4, 2])
+            for hd in range(2):
+                nc.tensor.matmul(
+                    bank[:, hd].rearrange("p k c -> p (k c)"), lhsT=pick[:, hd, :], rhs=rel_in[:], start=True, stop=True,
+                )
+            for c2 in range(2):
+                rows = slice(64 * c2, 64 * (c2 + 1))
+                nc.scalar.copy(out=rel_col[rows, :].rearrange("p (h k) -> p h k", h=2), in_=bank[rows, :, :, c2])
 
-        def h_run(i):
-            if i == 0:
-                return
-            role, g, half = quads[i - 1]
-            for dt in (4 * half, 4 * half + 2):
-                ht(role, g, dt)
-            for n, dt in enumerate((4 * half, 4 * half + 2)):
-                tt(role, g, dt, TT_ENG[2 * i + n])
+        a_blocks = [(role, g, rows) for role in (HEAD, TAIL) for rows in range(4) for g in range(2)]
+        tiles = [(hd, k, ph) for hd in range(2) for ph in range(2) for k in range(4)]
 
-        def mm_run(i, d0):
-            role, g, half = quads[i]
-            for dt in (4 * half + d0, 4 * half + d0 + 1):
-                mm(role, g, dt)
-            for dt in (4 * half + d0, 4 * half + d0 + 1):
-                th(role, g, dt)
+        def run_a(blocks):
+            for block in blocks:
+                a_turn(*block)
+            for block in blocks:
+                a_rows(*block)
 
-        def gm_at(i, d0):
-            role, g, half = quads[i]
-            gm(role, g, 4 * half + d0)
+        def run_units(role, g, units):
+            for dt in units:
+                unit_matmul(role, g, dt)
+            for dt in units:
+                unit_tanh(role, g, dt)
 
-        first = 0
-        for i in range(9):
-            mine = halves[first:first + EH_COUNT[i]]
-            first += EH_COUNT[i]
+        def turn_h(i):
+            role, g, hd = SLOTS[i]
+            for dt in (4 * hd, 4 * hd + 2):
+                pair_turn(role, g, dt)
+            for dt in (4 * hd, 4 * hd + 2):
+                pair_rows(role, g, dt, (i, dt - 4 * hd) in H_ON_VECTOR)
 
-            def eh_run():
-                for ph, c in mine:
-                    pm(0, c, ph)
-                for ph, c in mine:
-                    es(c, ph)
+        def run_eh(now):
+            for tile in now:
+                pooled(HEAD, *tile)
+            for tile in now:
+                eh_rel(*tile)
 
-            if i < 8:
-                mm_run(i, 0)
-                if HT_LATE[i] == 0:
-                    h_run(i)
-                a_run(3 * i)
-                if i < 6:
-                    dm(DM[6 + 2 * i])
-                mm_run(i, 2)
-                eh_run()
-                if i < 6:
-                    dm(DM[7 + 2 * i])
-                if i == GP_SLOT:
-                    for g in range(2):
-                        gp(1, g)
-                        gb(1, g)
-                for u in range(2):
-                    if X1_SLOT[u] == i:
-                        x1(u)
-                        dm(DM[4 + u])
-                if GM_FIRST:
-                    gm_at(i, 0)
-                if HT_LATE[i] == 1:
-                    h_run(i)
-                a_run(3 * i + 1)
-                if i == max(0, max(X1_SLOT) + XQ_LAG):
-                    xq(1, 0)
-                    xq(1, 1)
-                if not GM_FIRST:
-                    gm_at(i, 0)
-                gm_at(i, 2)
+        def run_et(now):
+            for tile in now:
+                pooled(TAIL, *tile)
+            for tile in now:
+                product(*tile)
+
+        def run_sums(now):
+            for hd, ph in now:
+                sum_turn(hd, ph)
+            for hd, ph in now:
+                finish(hd, ph)
+
+        a_done, eh_done, et_done = 0, 0, 0
+        summable = []
+        for i in range(len(EH_TILES)):
+            eh_now = tiles[eh_done:eh_done + EH_TILES[i]]
+            et_now = tiles[et_done:et_done + ET_TILES[i]]
+            eh_done += len(eh_now)
+            et_done += len(et_now)
+            if i < len(SLOTS):
+                role, g, hd = SLOTS[i]
+                between = a_blocks[a_done:a_done + A_BETWEEN[i]]
+                a_done += len(between)
+                behind = a_blocks[a_done:a_done + A_BEHIND[i]]
+                a_done += len(behind)
+
+                run_units(role, g, (4 * hd, 4 * hd + 1))
+                if i in H_EARLY:
+                    turn_h(i - 1)
+                run_a(between)
+                run_units(role, g, (4 * hd + 2, 4 * hd + 3))
+                run_eh(eh_now)
+                if i == 0:
+                    for gain_pass in range(2):
+                        gain_spread(TAIL, gain_pass)
+                if i == 2:
+                    rel_columns()
+                pair_gain(role, g, 4 * hd)
+                run_et(et_now)
+                if i > 0 and i not in H_EARLY:
+                    turn_h(i - 1)
+                run_a(behind)
+                run_sums(summable)
+                if i == 0:
+                    for kk in range(2):
+                        x_quant(1, kk)
+                pair_gain(role, g, 4 * hd + 2)
+                for w_role, quarter in W_PREP[i]:
+                    for kk in range(2):
+                        w_rows(w_role, kk, quarter)
+                    w_quant(w_role, quarter)
             else:
-                h_run(i)
-                eh_run()
-            for role in range(2):
-                for q in range(4):
-                    if W_SLOT[4 * role + q] == i:
-                        for kk in range(2):
-                            wi(role, kk, q, W_ENG[8 * role + 2 * q + kk])
-                    if W_SLOT[4 * role + q] >= 0 and W_SLOT[4 * role + q] + WQ_LAG == i:
-                        wq(role, q)
-            if i >= 1 and quads[i - 1][2] == 1:
-                role, g, half = quads[i - 1]
-                for ch in range(2):
-                    hq(role, g, ch)
-            for role in range(2):
-                for ph in range(2):
-                    for g in range(2):
-                        last = max(AT_SLOT[8 * role + 2 * pp + g] for pp in (2 * ph, 2 * ph + 1)) // 3
-                        if last + AQ_LAG == i:
-                            aq(role, g, ph)
-        done = 0
-        before = []
-        for n in SUM_RUNS + (0,):
-            now = halves[done:done + n]
-            done += n
-            for ph, c in now:
-                pm(1, c, ph)
-            for ph, c in now:
-                ev(c, ph)
-                if c % 2 == 1 and (c // 2, ph) in PAIRS:
-                    pair(c, ph)
-            for ph, c in before:
-                st(c, ph)
-                if c == C - 1:
-                    fin(ph)
-            before = now
+                if i == len(SLOTS):
+                    turn_h(i - 1)
+                run_eh(eh_now)
+                run_et(et_now)
+                run_sums(summable)
+            summable = [(hd, ph) for hd, k, ph in et_now if k == 3]
+            if 1 <= i <= len(SLOTS):
+                h_quant(*SLOTS[i - 1])
+            if i < len(SLOTS):
+                for block_role, block_g, rows in between + behind:
+                    if rows % 2 == 1:
+                        a_quant(block_role, block_g, rows // 2)

from contextlib import ExitStack

import concourse.mybir as mybir
from concourse.masks import make_identity

T, K, D, R = 1024, 1024, 1024, 128
C = D // R
FLOPS = 4 * 2 * 1024 * 1024 * 1024

F32 = mybir.dt.float32
BF16 = mybir.dt.bfloat16
U32 = mybir.dt.uint32
U8 = mybir.dt.uint8
FP8 = mybir.dt.float8_e4m3fn
FP8X4 = mybir.dt.float8_e4m3fn_x4
ACT = mybir.ActivationFunctionType
ALU = mybir.AluOpType

HEAD, TAIL = 0, 1

SLOTS = (
    (HEAD, 0, 0), (HEAD, 1, 0), (TAIL, 0, 0), (TAIL, 1, 0), (HEAD, 0, 1), (HEAD, 1, 1), (TAIL, 0, 1), (TAIL, 1, 1),
)
H_EARLY = (1, 5, 7)
A_BETWEEN = (2, 0, 2, 0, 0, 0, 2, 0)
A_BEHIND = (2, 4, 2, 1, 1, 0, 0, 0)
W_PREP = (
    ((TAIL, 0), (TAIL, 1)), ((HEAD, 3),), ((HEAD, 2),), ((TAIL, 2),), ((TAIL, 3),), (), (), (),
)
EH_TILES = (0, 0, 0, 0, 5, 3, 0, 5, 0, 2, 1, 0)
ET_TILES = (0, 0, 0, 0, 0, 2, 0, 0, 0, 7, 7, 0)
LOADS = (
    ("w", TAIL, 0, 0), ("w", TAIL, 1, 0), ("a", HEAD, 0), ("a", HEAD, 1), ("a", HEAD, 2), ("a", HEAD, 3),
    ("w", HEAD, 0, 1), ("w", HEAD, 1, 1), ("a", TAIL, 0), ("a", TAIL, 1), ("a", TAIL, 2), ("a", TAIL, 3),
    ("w", TAIL, 0, 1), ("w", TAIL, 1, 1),
)

W_ON_SCALAR = ((HEAD, 0, 0), (HEAD, 1, 0), (HEAD, 0, 1), (HEAD, 1, 2), (TAIL, 0, 1))
H_ON_VECTOR = ((1, 0), (4, 0), (4, 2), (6, 0), (7, 0))
A_ON_VECTOR = ((HEAD, 1, 3),)


def tile_relation_trilinear_score_f4_kernel(
    tc, x_bytes, x_scale, w_head, b_head, g_head, a_head, w_tail, b_tail, g_tail, a_tail, rel, beta, out
):
    nc = tc.nc
    w_in, b_in, g_in, a_in = (w_head, w_tail), (b_head, b_tail), (g_head, g_tail), (a_head, a_tail)

    with ExitStack() as ctx:
        keep = ctx.enter_context(tc.tile_pool(name="keep", bufs=1))
        work = ctx.enter_context(tc.tile_pool(name="work", bufs=2))
        psum = ctx.enter_context(tc.psum_pool(name="psum", bufs=4))

        def raw_tile(shape, dtype, nm):
            return work.tile(shape, dtype, name=nm, tag="raw", bufs=10, align_bytes=64)

        def big_tile(shape, dtype, nm):
            return work.tile(shape, dtype, name=nm, tag="big", bufs=8, align_bytes=64)

        def product_bank():
            return psum.tile([128, 512], F32, name="product", tag="product", bufs=4)

        def turn_bank(shape, dtype=F32):
            return psum.tile(shape, dtype, name="turn", tag="turn", bufs=4)

        scale_in = keep.tile([128, 2, 4], F32, name="scale_in")
        nc.scalar.dma_start(out=scale_in[:], in_=x_scale.rearrange("o (k p t) -> p (o k) t", k=2, p=128))
        zeros = keep.tile([128, 512], BF16, name="zeros")
        nc.vector.memset(zeros[:], 0.0)
        gain_rows = keep.tile([128, T], BF16, name="gain_rows")
        nc.vector.memset(gain_rows[:], 0.0)
        first_tanh = keep.tile([128, 1], F32, name="first_tanh")
        nc.vector.memset(first_tanh[:], 0.0)
        nc.scalar.activation(out=first_tanh[:], in_=first_tanh[:], func=ACT.Tanh)
        bias_rows = keep.tile([128, 128], BF16, name="bias_rows")
        nc.vector.memset(bias_rows[:], 0.0)

        x_in = [keep.tile([128, 4, K], U8, name="x_in%d" % g) for g in range(2)]
        x_view = x_bytes.rearrange("(g p j) k -> g p j k", p=128, j=4)
        w_raw, a_raw = {}, {}

        def load_x(g, u):
            nc.sync.dma_start(out=x_in[g][:, 2 * u:2 * u + 2, :], in_=x_view[g, :, 2 * u:2 * u + 2, :])

        def load_w(role, kk, dh):
            t = raw_tile([128, 4, 512], BF16, "w_raw")
            view = w_in[role][512 * kk:512 * (kk + 1), 512 * dh:512 * (dh + 1)]
            nc.sync.dma_start(out=t[:], in_=view.rearrange("(p j) d -> p j d", j=4))
            w_raw[role, kk, dh] = t

        def load_a(role, rows):
            t = raw_tile([128, 2, T], BF16, "a_raw")
            view = a_in[role][256 * rows:256 * (rows + 1), :]
            nc.sync.dma_start(out=t[:], in_=view.rearrange("(s p) t -> p s t", p=128))
            a_raw[role, rows] = t

        load_x(0, 0)
        load_x(0, 1)
        load_w(HEAD, 0, 0)
        load_w(HEAD, 1, 0)
        for role in (HEAD, TAIL):
            nc.sync.dma_start(out=gain_rows[role:role + 1, :], in_=g_in[role].rearrange("(o t) -> o t", o=1))
        for role in (HEAD, TAIL):
            nc.sync.dma_start(out=bias_rows[8 * role:8 * role + 8, :], in_=b_in[role].rearrange("(t q) -> t q", q=128))
        load_x(1, 0)
        load_x(1, 1)
        rel_in = keep.tile([128, C], BF16, name="rel_in")
        nc.sync.dma_start(out=rel_in[:], in_=rel)

        ident = keep.tile([128, 128], F32, name="ident")
        make_identity(nc, ident[:])
        ident_bf = keep.tile([128, 128], BF16, name="ident_bf")
        make_identity(nc, ident_bf[:])
        pick = keep.tile([128, 2, 128], BF16, name="pick")
        for hd in range(2):
            nc.gpsimd.tensor_copy(
                out=pick[:, hd, :].rearrange("p (c r) -> p c r", c=2),
                in_=ident_bf[:, 64 * hd:64 * (hd + 1)].unsqueeze(1).to_broadcast([128, 2, 64]),
            )
        beta_row = keep.tile([128, 2, 128], BF16, name="beta_row")
        nc.gpsimd.memset(beta_row[:], 0.0)

        scale_x = keep.tile([128, 2, 2, 4], F32, name="scale_x")
        bias = keep.tile([128, 16], BF16, name="bias")
        rel_col = keep.tile([128, 8], F32, name="rel_col")

        for load in LOADS:
            if load[0] == "w":
                load_w(*load[1:])
            else:
                load_a(*load[1:])
        nc.sync.dma_start(out=beta_row[0:1, :, 0:64], in_=beta.rearrange("(o h r) -> o h r", o=1, h=2))

        made = {}

        def codes(nm, bufs=1):
            c = keep.tile([128, 512], U32, name=nm + "_codes", align_bytes=64, bufs=bufs)
            s = keep.tile([128, 512], U8, name=nm + "_scales", align_bytes=64, bufs=bufs)
            return c, s

        def quantize(dst, src):
            nc.vector.quantize_mx(out=dst[0][:].bitcast(FP8X4), scales=dst[1][:], in_=src)

        def mx_pass(acc, lhs, col, rhs, g):
            cols = slice(col, col + 128)
            nc.tensor.matmul_mx(
                out=acc[:], lhsT=lhs[0][:, cols].bitcast(FP8X4), lhsT_scale=lhs[1][:, cols],
                rhs=rhs[0][:].bitcast(FP8X4), rhs_scale=rhs[1][:], start=(g == 0), stop=(g == 1),
            )

        def copy(on_vector, dst, src):
            if on_vector:
                nc.vector.tensor_copy(out=dst, in_=src)
            else:
                nc.scalar.copy(out=dst, in_=src)

        def row_to_all(row):
            return ident_bf[:, row:row + 1].to_broadcast([128, 128])

        def warm(n):
            bank = product_bank()
            for k in range(n):
                nc.tensor.matmul(bank[:], lhsT=zeros[:, 0:128], rhs=zeros[:], start=True, stop=True)

        def x_widen(g, u, on_vector):
            t = big_tile([128, 2, K], BF16, "x_wide")
            src = x_in[g][:, 2 * u:2 * u + 2, :].rearrange("p e k -> p (e k)").bitcast(FP8)
            copy(on_vector, t[:].rearrange("p e k -> p (e k)"), src)
            made["x_wide", g, u] = t

        def x_turn(g, u, kk):
            bank = turn_bank([128, 2, 2, 128])
            for e in range(2):
                words = made["x_wide", g, u][:, e, :].bitcast(F32)
                for v in range(2):
                    nc.tensor.transpose(bank[:, e, v, :], words[:, 256 * kk + v:256 * (kk + 1):2], ident[:])
            made["x_turn", g, u, kk] = bank

        def x_scaled(g, u, kk):
            if u == 0:
                made["x_rows", g, kk] = big_tile([128, 2, 1024], BF16, "x_rows")
            bank = made["x_turn", g, u, kk][:].rearrange("p e v q -> p (e v q)").bitcast(BF16)
            scales = scale_x[:, kk].rearrange("p e t -> p (e t)").rearrange("p (w b) -> p w b", b=2)
            nc.vector.tensor_tensor(
                out=made["x_rows", g, kk][:, u, :].rearrange("p (q w b) -> p q w b", w=4, b=2),
                in0=bank.rearrange("p (w q b) -> p q w b", w=4, b=2),
                in1=scales.unsqueeze(1).to_broadcast([128, 128, 4, 2]),
                op=ALU.mult,
            )

        def x_quant(g, kk):
            made["x", g, kk] = codes("x%d%d" % (g, kk))
            quantize(made["x", g, kk], made["x_rows", g, kk][:].rearrange("p u n -> p (u n)"))

        def gain_spread(role, g):
            bank = turn_bank([128, 512])
            nc.tensor.matmul(
                bank[:], lhsT=row_to_all(role), rhs=gain_rows[:, 512 * g:512 * (g + 1)], start=True, stop=True,
            )
            t = keep.tile([128, 512], BF16, name="gain%d%d" % (role, g), align_bytes=64)
            nc.scalar.copy(
                out=t[:].rearrange("p (u q e) -> p u q e", u=2, e=2),
                in_=bank[:].rearrange("p (q u e) -> p u q e", u=2, e=2),
            )
            made["gain", role, g] = t

        def w_rows(role, kk, quarter):
            if kk == 0:
                made["w_rows", role, quarter] = work.tile(
                    [128, 2, 256, 4], BF16, name="w_rows", tag="w_rows", bufs=3, align_bytes=64,
                )
            d0 = 256 * (quarter % 2)
            src = w_raw[role, kk, quarter // 2][:, :, d0:d0 + 256].rearrange("p j d -> p d j")
            copy((role, kk, quarter) not in W_ON_SCALAR, made["w_rows", role, quarter][:, kk], src)

        def w_quant(role, quarter):
            made["w", role, quarter] = codes("w%d" % quarter, bufs=2)
            quantize(made["w", role, quarter], made["w_rows", role, quarter][:].rearrange("p k d j -> p (k d j)"))

        def a_turn(role, g, rows):
            words = a_raw[role, rows][:].rearrange("p s t -> p (s t)").bitcast(F32)
            bank = turn_bank([128, 2, 2, 128])
            for s in range(2):
                for u in range(2):
                    w0 = 512 * s + 256 * g
                    nc.tensor.transpose(bank[:, s, u, :], words[:, w0 + u:w0 + 256:2], ident[:])
            made["a_turn", role, g, rows] = bank

        def a_rows(role, g, rows):
            if rows % 2 == 0:
                made["a_rows", role, g, rows // 2] = work.tile(
                    [128, 512, 4], BF16, name="a_rows", tag="a_rows", bufs=4, align_bytes=64,
                )
            dst = made["a_rows", role, g, rows // 2][:].rearrange("p n t -> p (n t)").bitcast(F32)
            dst = dst.rearrange("p (s r u) -> p s r u", s=4, u=2)[:, 2 * (rows % 2):2 * (rows % 2) + 2]
            src = made["a_turn", role, g, rows][:].rearrange("p s u r -> p s r u")
            copy((role, g, rows) in A_ON_VECTOR, dst, src)

        def a_quant(role, g, ph):
            made["a", role, g, ph] = codes("a%d%d%d" % (role, g, ph))
            quantize(made["a", role, g, ph], made["a_rows", role, g, ph][:].rearrange("p n t -> p (n t)"))

        def unit_matmul(role, g, dt):
            acc = product_bank()
            for kk in range(2):
                mx_pass(acc, made["w", role, dt // 2], 256 * kk + 128 * (dt % 2), made["x", g, kk], kk)
            made["unit", role, g, dt] = acc

        def unit_tanh(role, g, dt):
            first = dt - dt % 2
            if dt == first:
                made["tanh", role, g, first] = work.tile([128, 2, 512], F32, name="tanh", tag="tanh", bufs=4)
            col = 8 * role + dt
            nc.scalar.activation(
                out=made["tanh", role, g, first][:, dt - first, :], in_=made["unit", role, g, dt][:], func=ACT.Tanh,
                bias=bias[:, col:col + 1],
            )

        def pair_gain(role, g, dt):
            t = work.tile([128, 2, 512], BF16, name="h_cols", tag="h_cols", bufs=4, align_bytes=64)
            gain = made["gain", role, g][:].unsqueeze(1).to_broadcast([128, 2, 512])
            nc.vector.tensor_tensor(out=t[:], in0=made["tanh", role, g, dt][:], in1=gain, op=ALU.mult)
            made["h_cols", role, g, dt] = t

        def pair_turn(role, g, dt):
            bank = turn_bank([128, 2, 256])
            for s in range(2):
                words = made["h_cols", role, g, dt][:, s, :].bitcast(F32)
                for u in range(2):
                    nc.tensor.transpose(bank[:, u, 128 * s:128 * (s + 1)], words[:, 128 * u:128 * (u + 1)], ident[:])
            made["h_turn", role, g, dt] = bank

        def pair_rows(role, g, dt, on_vector):
            hd = dt // 4
            if dt % 4 == 0:
                made["h_rows", role, g, hd] = work.tile(
                    [128, C, 64, 4], BF16, name="h_rows", tag="h_rows", bufs=4, align_bytes=64,
                )
            dst = made["h_rows", role, g, hd][:].rearrange("p c r t -> p (c r t)").bitcast(F32)
            r0 = 16 * (dt % 4)
            dst = dst.rearrange("p (c r u) -> p c r u", c=C, u=2)[:, :, r0:r0 + 32, :]
            copy(on_vector, dst, made["h_turn", role, g, dt][:].rearrange("p u (r c) -> p c r u", c=C))

        def h_quant(role, g, hd):
            made["h", role, g, hd] = codes("h%d%d%d" % (role, g, hd))
            quantize(made["h", role, g, hd], made["h_rows", role, g, hd][:].rearrange("p c r t -> p (c r t)"))

        def pooled(role, hd, k, ph):
            acc = product_bank()
            for g in range(2):
                mx_pass(acc, made["h", role, g, hd], 128 * k, made["a", role, g, ph], g)
            made["pooled", role, hd, k, ph] = acc

        def eh_rel(hd, k, ph):
            if ph == 0:
                made["eh", hd, k] = big_tile([128, 2, 512], F32, "eh")
            col = 4 * hd + k
            nc.scalar.activation(
                out=made["eh", hd, k][:, ph, :], in_=made["pooled", HEAD, hd, k, ph][:], func=ACT.Copy,
                scale=rel_col[:, col:col + 1],
            )

        def added_early(hd, k, ph):
            return (hd, k, ph) != (1, 2, 1)

        def product(hd, k, ph):
            first = k - k % 2
            if k == first:
                made["product", hd, first, ph] = raw_tile([128, 2, 512], F32, "product")
            t = made["product", hd, first, ph]
            nc.vector.tensor_tensor(
                out=t[:, k - first, :], in0=made["pooled", TAIL, hd, k, ph][:], in1=made["eh", hd, first + k % 2][:, ph, :],
                op=ALU.mult,
            )
            if k > first and added_early(hd, first, ph):
                nc.gpsimd.tensor_tensor(out=t[:, 0, :], in0=t[:, 0, :], in1=t[:, 1, :], op=ALU.add)

        def sum_turn(hd, ph):
            terms = []
            for k in (0, 2):
                t = made["product", hd, k, ph]
                terms.append(t[:, 0, :])
                if not added_early(hd, k, ph):
                    terms.append(t[:, 1, :])
            bank = turn_bank([128, 4, 128])
            nc.tensor.matmul(
                bank[:], lhsT=row_to_all(0), rhs=beta_row[:, hd, :].unsqueeze(1).to_broadcast([128, 4, 128]),
                start=True, stop=False,
            )
            for m in range(4):
                for n in range(len(terms)):
                    nc.tensor.matmul(
                        bank[:, m, :], lhsT=terms[n][:, 128 * m:128 * (m + 1)], rhs=ident[:],
                        is_transpose=True, start=False, stop=(m == 3 and n == len(terms) - 1),
                    )
            made["sum", hd, ph] = bank

        def finish(hd, ph):
            t = work.tile([128, 4, 64], F32, name="score", tag="score", bufs=2)
            nc.vector.tensor_reduce(
                out=t[:], in_=made["sum", hd, ph][:].rearrange("p m (c r) -> p m r c", c=2),
                axis=mybir.AxisListType.X, op=ALU.add,
            )
            dst = out[512 * ph:512 * (ph + 1), 64 * hd:64 * (hd + 1)]
            nc.sync.dma_start(out=dst.rearrange("(m p) r -> p m r", p=128), in_=t[:])

        ctx.enter_context(tc.manual_schedule())

        warm(6)
        x_widen(0, 0, True)
        x_widen(0, 1, False)
        nc.vector.tensor_copy(out=scale_x[:], in_=scale_in[:].unsqueeze(2).to_broadcast([128, 2, 2, 4]))
        for kk in range(2):
            for u in range(2):
                x_turn(0, u, kk)
        for kk in range(2):
            w_rows(HEAD, kk, 0)
        for kk in range(2):
            if kk == 1:
                x_widen(1, 0, False)
                w_rows(HEAD, 0, 1)
                w_rows(HEAD, 1, 1)
            for u in range(2):
                x_scaled(0, u, kk)
            x_quant(0, kk)
            w_quant(HEAD, kk)
        x_widen(1, 1, False)
        bias_bank = turn_bank([128, 128], BF16)
        nc.tensor.transpose(bias_bank[:], bias_rows[:], ident_bf[:])
        nc.scalar.copy(out=bias[:], in_=bias_bank[:, 0:16])
        for g in range(2):
            gain_spread(HEAD, g)
        warm(1)
        for u in range(2):
            for kk in range(2):
                x_turn(1, u, kk)
            for kk in range(2):
                x_scaled(1, u, kk)
            if u == 0:
                warm(2)

        def rel_columns():
            bank = turn_bank([128, 2, 4, 2])
            for hd in range(2):
                nc.tensor.matmul(
                    bank[:, hd].rearrange("p k c -> p (k c)"), lhsT=pick[:, hd, :], rhs=rel_in[:], start=True, stop=True,
                )
            for c2 in range(2):
                rows = slice(64 * c2, 64 * (c2 + 1))
                nc.scalar.copy(out=rel_col[rows, :].rearrange("p (h k) -> p h k", h=2), in_=bank[rows, :, :, c2])

        a_blocks = [(role, g, rows) for role in (HEAD, TAIL) for rows in range(4) for g in range(2)]
        tiles = [(hd, k, ph) for hd in range(2) for ph in range(2) for k in range(4)]

        def run_a(blocks):
            for block in blocks:
                a_turn(*block)
            for block in blocks:
                a_rows(*block)

        def run_units(role, g, units):
            for dt in units:
                unit_matmul(role, g, dt)
            for dt in units:
                unit_tanh(role, g, dt)

        def turn_h(i):
            role, g, hd = SLOTS[i]
            for dt in (4 * hd, 4 * hd + 2):
                pair_turn(role, g, dt)
            for dt in (4 * hd, 4 * hd + 2):
                pair_rows(role, g, dt, (i, dt - 4 * hd) in H_ON_VECTOR)

        def run_eh(now):
            for tile in now:
                pooled(HEAD, *tile)
            for tile in now:
                eh_rel(*tile)

        def run_et(now):
            for tile in now:
                pooled(TAIL, *tile)
            for tile in now:
                product(*tile)

        def run_sums(now):
            for hd, ph in now:
                sum_turn(hd, ph)
            for hd, ph in now:
                finish(hd, ph)

        a_done, eh_done, et_done = 0, 0, 0
        summable = []
        for i in range(len(EH_TILES)):
            eh_now = tiles[eh_done:eh_done + EH_TILES[i]]
            et_now = tiles[et_done:et_done + ET_TILES[i]]
            eh_done += len(eh_now)
            et_done += len(et_now)
            if i < len(SLOTS):
                role, g, hd = SLOTS[i]
                between = a_blocks[a_done:a_done + A_BETWEEN[i]]
                a_done += len(between)
                behind = a_blocks[a_done:a_done + A_BEHIND[i]]
                a_done += len(behind)

                run_units(role, g, (4 * hd, 4 * hd + 1))
                if i in H_EARLY:
                    turn_h(i - 1)
                run_a(between)
                run_units(role, g, (4 * hd + 2, 4 * hd + 3))
                run_eh(eh_now)
                if i == 0:
                    for gain_pass in range(2):
                        gain_spread(TAIL, gain_pass)
                if i == 2:
                    rel_columns()
                pair_gain(role, g, 4 * hd)
                run_et(et_now)
                if i > 0 and i not in H_EARLY:
                    turn_h(i - 1)
                run_a(behind)
                run_sums(summable)
                if i == 0:
                    for kk in range(2):
                        x_quant(1, kk)
                pair_gain(role, g, 4 * hd + 2)
                for w_role, quarter in W_PREP[i]:
                    for kk in range(2):
                        w_rows(w_role, kk, quarter)
                    w_quant(w_role, quarter)
            else:
                if i == len(SLOTS):
                    turn_h(i - 1)
                run_eh(eh_now)
                run_et(et_now)
                run_sums(summable)
            summable = [(hd, ph) for hd, k, ph in et_now if k == 3]
            if 1 <= i <= len(SLOTS):
                h_quant(*SLOTS[i - 1])
            if i < len(SLOTS):
                for block_role, block_g, rows in between + behind:
                    if rows % 2 == 1:
                        a_quant(block_role, block_g, rows // 2)
